import numpy as np
import ml_dtypes


def mxq(x, axis, fmt="e4m3"):
    dtype, down = {"e4m3": (ml_dtypes.float8_e4m3fn, 7), "e5m2": (ml_dtypes.float8_e5m2, 14)}[fmt]
    v = np.moveaxis(np.asarray(x, np.float32).astype(ml_dtypes.bfloat16).astype(np.float64), axis, -1)
    blocks = v.reshape(v.shape[:-1] + (-1, 32))
    amax = np.abs(blocks).max(-1, keepdims=True)
    byte = np.maximum(np.where(amax > 0, np.frexp(amax)[1] - 1 + 127, 0) - down, 1)
    scale = np.exp2(byte - 127.0)
    codes = (blocks / scale).astype(np.float32).astype(dtype).astype(np.float64)
    return np.moveaxis((codes * scale).reshape(v.shape), -1, axis)


WIDE = False


def mx_kscale(k):
    if not WIDE:
        return np.ones(k)
    levels = np.array([10, -10, 5, -5, 0])
    if k % 512:
        return np.exp2(np.random.permutation(np.resize(levels, k // 32))).repeat(32)
    a = np.empty((k // 512, 16))
    for p in range(k // 512):
        a[p, :8] = np.random.permutation(np.resize(levels, 8))
        for g in range(8):
            far = levels[np.abs(levels - a[p, g]) >= 10]
            a[p, g + 8] = far[np.random.randint(len(far))]
    return np.exp2(a.ravel()).repeat(32)


BF16 = ml_dtypes.bfloat16


def bf(x):
    return np.asarray(x, np.float32).astype(BF16)


def f64(x):
    return np.asarray(x).astype(np.float64)


E2M1 = np.array([0.0, 0.5, 1.0, 1.5, 2.0, 3.0, 4.0, 6.0, -0.0, -0.5, -1.0, -1.5, -2.0, -3.0, -4.0, -6.0])


def pack_weight(w, fmt):
    k, n = w.shape
    w = f64(bf(w)).reshape(k // 32, 32, n)
    amax = np.abs(w).max(1)
    if fmt == "e4m3":
        byte = np.frexp(amax)[1] - 1 + 127 - 7
    else:
        mant, ex = np.frexp(amax / 6.0)
        byte = np.where(mant > 0.5, ex, ex - 1) + 127
    byte = np.clip(np.where(amax > 0, byte, 1), 1, 254)
    scaled = (w * np.exp2(127.0 - byte)[:, None, :]).reshape(k, n).astype(np.float32)
    by_word = np.ascontiguousarray(scaled.reshape(k // 512, 128, 4, n).transpose(0, 1, 3, 2))
    if fmt == "e4m3":
        words = by_word.astype(ml_dtypes.float8_e4m3fn).view(np.uint8)
    else:
        c = by_word.astype(ml_dtypes.float4_e2m1fn).view(np.uint8) & 0xF
        words = c[..., 0::2] | (c[..., 1::2] << 4)
    return np.ascontiguousarray(words), np.ascontiguousarray(byte.astype(np.uint8).reshape(k // 512, 16, n))


def unpack_weight(words, scales, fmt):
    g, p, n, _ = words.shape
    if fmt == "e4m3":
        vals = np.ascontiguousarray(words).view(ml_dtypes.float8_e4m3fn).astype(np.float64)
    else:
        nib = np.empty((g, p, n, 4), np.uint8)
        nib[..., 0::2] = words & 0xF
        nib[..., 1::2] = words >> 4
        vals = E2M1[nib]
    vals = vals * np.repeat(np.exp2(scales.astype(np.float64) - 127.0), 8, axis=1)[..., None]
    return vals.transpose(0, 1, 3, 2).reshape(g * 512, n)
def pack4(w):
    words, scales = pack_weight(w, "e2m1")
    return words.reshape(words.shape[0], 128, -1), scales


def unpack4(words, scales):
    return unpack_weight(words.reshape(words.shape[0], 128, -1, 2), scales, "e2m1")


P, N, T = 1024, 1024, 1024

CONC = 0.25


def draw0():
    s, t = mx_kscale(N), mx_kscale(N)
    signals = np.random.standard_normal((P, N)) * s
    u = np.random.standard_normal((N, N)) / np.sqrt(N) / s[:, None] * t
    u_words, u_scales = pack4(u)
    lam = np.random.uniform(0.7, 1.3, N)
    tilt = 1.0 + 0.1 * np.random.standard_normal(N)
    q = np.random.standard_normal((T, N)) / np.sqrt(N) / t
    return {"signals": bf(signals), "u_words": u_words, "u_scales": u_scales, "lam": bf(lam), "tilt": bf(tilt), "q": bf(q)}


def qis_eigenvalues(lam):
    n = lam.shape[0]
    c = CONC
    h = (c ** 2) ** 0.35 * float(n) ** (-0.35)
    l = 1.0 / lam
    l_j = l[:, None]
    d = l_j - l[None, :]
    den = d ** 2 + h ** 2 * l_j ** 2
    theta = np.mean(l_j * d / den, axis=0)
    eta = np.mean(h * l_j ** 2 / den, axis=0)
    amp2 = theta ** 2 + eta ** 2
    r = 1.0 / (l * ((1.0 - c) ** 2 + 2.0 * c * (1.0 - c) * theta + c ** 2 * amp2))
    return r * np.sum(lam) / np.sum(r)


def core(signals, u_words, u_scales, lam, tilt, q):
    delta = qis_eigenvalues(f64(lam))
    y = mxq(f64(signals), 1, "e4m3") @ unpack4(u_words, u_scales)
    x = y * f64(tilt)[None, :] / delta[None, :]
    return mxq(x, 1, "e4m3") @ mxq(f64(q), 1, "e4m3").T


def e4m3fn_bytes(y):
    return np.clip(np.asarray(y, np.float64), -448.0, 448.0).astype(np.float32).astype(ml_dtypes.float8_e4m3fn).view(np.uint8)


def e4m3fn_values(b):
    return np.asarray(b, np.uint8).view(ml_dtypes.float8_e4m3fn).astype(np.float64)


def setup_inputs():
    d = draw0()
    x0 = np.asarray(d['signals']).astype(np.float64)
    s = (np.max(np.abs(x0), axis=(0,), keepdims=True) / 448.0).astype(np.float32)
    out = {}
    for k, v in d.items():
        if k == 'signals':
            out['signals_bytes'] = e4m3fn_bytes(x0 / s.astype(np.float64))
            out['signals_scale'] = s
        else:
            out[k] = v
    return out


def reference(signals_bytes, signals_scale, u_words, u_scales, lam, tilt, q):
    return core(e4m3fn_values(signals_bytes) * signals_scale.astype(np.float64), u_words, u_scales, lam, tilt, q)

@@ -1,0 +1,542 @@
+from contextlib import ExitStack
+
+import concourse.mybir as mybir
+from concourse.masks import make_identity
+
+F32 = mybir.dt.float32
+BF16 = mybir.dt.bfloat16
+I32 = mybir.dt.int32
+U32 = mybir.dt.uint32
+U8 = mybir.dt.uint8
+FP8 = mybir.dt.float8_e4m3fn
+FP8X4 = mybir.dt.float8_e4m3fn_x4
+FP4X4 = mybir.dt.float4_e2m1fn_x4
+ALU = mybir.AluOpType
+ACT = mybir.ActivationFunctionType
+
+P = 128
+N = 1024
+CONC = 0.25
+H = (CONC**2) ** 0.35 * float(N) ** (-0.35)
+WARM = (5, 2, 1)
+FLOPS = 2 * 2 * N * N * N
+
+
+def tile_quadraticinverseshrinkagesignalpnl_w4_kernel(
+    tc, signals_bytes, signals_scale, u_words, u_scales, lam, tilt, q, out
+):
+    nc = tc.nc
+    with ExitStack() as ctx:
+        keep = ctx.enter_context(tc.tile_pool(name="keep", bufs=1))
+        ring = ctx.enter_context(tc.tile_pool(name="ring", bufs=3))
+        psum = ctx.enter_context(tc.psum_pool(name="psum", bufs=1))
+        ctx.enter_context(tc.manual_schedule())
+
+        def bank(b, shape):
+            return psum.tile(shape, F32, name="bank", tag="bank%d" % b)
+
+        lam_c = keep.tile([P, 8], BF16, name="lam_c")
+        scale_c = keep.tile([P, 8], F32, name="scale_c")
+        tilt_c = keep.tile([P, 8], BF16, name="tilt_c")
+        q_raw = [keep.tile([P, 2, N], BF16, name="q_raw%d" % d) for d in range(4)]
+        s_raw = [keep.tile([P, 2, N], U8, name="s_raw%d" % d) for d in range(4)]
+        uw_raw = keep.tile([P, 2, 2 * N], U8, name="uw_raw")
+        us_raw = keep.tile([P, 2, N], U8, name="us_raw")
+
+        ident = keep.tile([P, P], F32, name="ident")
+        ones = keep.tile([P, P], F32, name="ones")
+        nc.gpsimd.memset(ones[:], 1.0)
+        make_identity(nc, ident[:])
+
+        def stoke(count, bk=7):
+            b = bank(bk, [P, P])
+            for n in range(count):
+                nc.tensor.matmul(b[:], lhsT=ones[:], rhs=ones[:], start=True, stop=True)
+
+        stoke(WARM[0])
+
+        def load_q(d):
+            nc.sync.dma_start(out=q_raw[d][:], in_=q[256 * d : 256 * (d + 1), :].rearrange("(a p) k -> p a k", p=P))
+
+        def load_s(d):
+            nc.sync.dma_start(out=s_raw[d][:], in_=signals_bytes[256 * d : 256 * (d + 1), :].rearrange("(p a) k -> p a k", a=2))
+
+        nc.sync.dma_start(out=lam_c[:].rearrange("p (g t) -> p g t", g=2), in_=lam.rearrange("(g p t) -> p g t", g=2, t=4))
+        nc.sync.dma_start(out=scale_c[:].rearrange("p (g t) -> p g t", g=2), in_=signals_scale.rearrange("o (g p t) -> p (o g) t", g=2, t=4))
+        load_q(0)
+        load_s(0)
+        nc.sync.dma_start(out=tilt_c[:].rearrange("p (g t) -> p g t", g=2), in_=tilt.rearrange("(g p t) -> p g t", g=2, t=4))
+        load_q(1)
+        load_q(2)
+
+        warm = keep.tile([P, 2], F32, name="warm")
+        nc.vector.memset(warm[:, 0:1], 1.0)
+        nc.scalar.activation(out=warm[:, 1:2], in_=warm[:, 0:1], func=ACT.Abs_reciprocal_sqrt)
+
+        tab_a = keep.tile([P, 4, 16, 8, 2], BF16, name="tab_a")
+        tab_b = keep.tile([P, 4, 16, 8, 2], BF16, name="tab_b")
+        nc.vector.memset(us_raw[:].bitcast(I32), 0)
+        for tab in (tab_b, tab_a):
+            nc.vector.memset(tab[:].rearrange("p c l s e -> p (c l s e)").bitcast(I32), 0)
+        for tab, levels, slot, value in (
+            (tab_b, slice(0, 8), 0, 1.0),
+            (tab_b, slice(0, 4), 3, 2.0),
+            (tab_b, slice(4, 8), 3, 1.0),
+            (tab_b, slice(4, 8), 5, 1.0),
+            (tab_a, slice(0, 4), 4, 1.0),
+            (tab_a, slice(0, 4), 7, 2.0),
+            (tab_a, slice(4, 8), 7, 1.0),
+        ):
+            nc.vector.memset(tab[:, :, levels, slot, :], value)
+        nc.sync.dma_start(out=uw_raw[:].bitcast(I32), in_=u_words.rearrange("g p n -> p g n").bitcast(I32))
+        for quad in range(4):
+            nc.sync.dma_start(
+                out=us_raw[32 * quad : 32 * quad + 4].bitcast(I32),
+                in_=u_scales[:, 4 * quad : 4 * quad + 4, :].rearrange("g r n -> r g n").bitcast(I32),
+            )
+        load_s(1)
+        load_s(2)
+        load_q(3)
+        load_s(3)
+
+        words_a = tab_a[:].bitcast(F32).rearrange("p c l s o -> p c l (s o)")
+        words_b = tab_b[:].bitcast(F32).rearrange("p c l s o -> p c l (s o)")
+
+        base = keep.tile([P, 3, 8], F32, name="base")
+        hl = keep.tile([P, 2, 2, 8], BF16, name="hl")
+        z = keep.tile([P, 10, 8], F32, name="z")
+        rest = keep.tile([P, 10, 8], F32, name="rest")
+        y = keep.tile([P, 3, 10, 8], BF16, name="y")
+        lam32 = keep.tile([P, 8], F32, name="lam32")
+        lam_sum = keep.tile([P, 1], F32, name="lam_sum")
+        inv_lam = keep.tile([P, 8], F32, name="inv_lam")
+        arg_scale = keep.tile([P, 8], F32, name="arg_scale")
+        arg_bias = keep.tile([P, 8], F32, name="arg_bias")
+        h_lam = keep.tile([P, 8], F32, name="h_lam")
+        inv_total = keep.tile([P, 1], F32, name="inv_total")
+        weight = keep.tile([P, 8], F32, name="weight")
+        scale_row = keep.tile([P, N], F32, name="scale_row")
+
+        lam_pairs = lam_c[:].rearrange("p (c e) -> p c e", e=2)
+        for tab, levels, slot in ((tab_b, slice(0, 8), 1), (tab_b, slice(4, 8), 4), (tab_a, slice(0, 4), 5)):
+            count = levels.stop - levels.start
+            nc.scalar.activation(
+                out=tab[:, :, levels, slot, :],
+                in_=lam_pairs.unsqueeze(2).to_broadcast([P, 4, count, 2]),
+                func=ACT.Copy,
+                scale=-4.0,
+            )
+
+        scale_banks = []
+        for g in range(2):
+            sb = bank(g, [P, 4, P])
+            scale_banks.append(sb)
+            for t in range(4):
+                nc.tensor.transpose(sb[:, t, :], scale_c[:, 4 * g + t : 4 * g + t + 1].to_broadcast([P, P]), ident[:])
+
+        nc.vector.tensor_tensor(out=base[:, 1, :], in0=lam_c[:], in1=lam_c[:], op=ALU.mult)
+        nc.vector.scalar_tensor_tensor(out=base[:, 0, :], in0=lam_c[:], scalar=2.0 * H * H, in1=lam_c[:], op0=ALU.mult, op1=ALU.mult)
+        nc.vector.tensor_scalar(out=base[:, 2, :], in0=lam_c[:], scalar1=0.5, scalar2=None, op0=ALU.mult)
+        nc.vector.tensor_scalar(out=lam32[:], in0=lam_c[:], scalar1=1.0, scalar2=None, op0=ALU.mult, op1=ALU.add, accum_out=lam_sum[:])
+        nc.vector.tensor_copy(out=hl[:, 0], in_=base[:, 0:2, :])
+        nc.vector.tensor_tensor(out=z[:, 1, :], in0=base[:, 1, :], in1=lam_c[:], op=ALU.mult)
+        nc.vector.tensor_scalar(out=z[:, 2, :], in0=base[:, 1, :], scalar1=6.0, scalar2=None, op0=ALU.mult)
+        nc.vector.tensor_tensor(out=hl[:, 1], in0=base[:, 0:2, :], in1=hl[:, 0], op=ALU.subtract)
+        nc.vector.reciprocal(out=inv_lam[:], in_=lam32[:])
+        nc.vector.tensor_scalar(out=arg_bias[:], in0=base[:, 1, :], scalar1=(H * H * N / CONC) ** 2, scalar2=None, op0=ALU.mult)
+        nc.vector.tensor_tensor(out=z[:, 0:7:6, :], in0=hl[:, 0:1, 1, :].to_broadcast([P, 2, 8]), in1=hl[:, :, 1, :], op=ALU.mult)
+        nc.vector.tensor_tensor(out=z[:, 9, :], in0=hl[:, 1, 1, :], in1=hl[:, 1, 1, :], op=ALU.mult)
+        nc.vector.tensor_tensor(
+            out=z[:, 3:9, :].rearrange("p (i j) c -> p i j c", j=2)[:, 0:3:2],
+            in0=hl[:, :, 0:1, :].to_broadcast([P, 2, 2, 8]),
+            in1=base[:, 1:3, :].unsqueeze(1).to_broadcast([P, 2, 2, 8]),
+            op=ALU.mult,
+        )
+        nc.vector.tensor_tensor(out=z[:, 5, :], in0=hl[:, 0, 0, :], in1=hl[:, 1, 0, :], op=ALU.add)
+        nc.vector.tensor_copy(
+            out=words_b[:, :, 0:8, 2:7:4],
+            in_=hl[:, :, 1, :].bitcast(F32).rearrange("p s c -> p c s").unsqueeze(2).to_broadcast([P, 4, 8, 2]),
+        )
+        nc.vector.tensor_copy(out=y[:, 0], in_=z[:])
+        nc.vector.scalar_tensor_tensor(out=arg_scale[:], in0=inv_lam[:], scalar=(N / CONC) ** 2, in1=inv_lam[:], op0=ALU.mult, op1=ALU.mult)
+        nc.vector.tensor_scalar(out=h_lam[:], in0=lam_c[:], scalar1=H, scalar2=None, op0=ALU.mult)
+        nc.vector.tensor_tensor(out=y[:, 1], in0=z[:], in1=y[:, 0], op=ALU.subtract)
+        nc.vector.tensor_tensor(out=rest[:], in0=z[:], in1=y[:, 0], op=ALU.subtract)
+
+        nc.vector.tensor_tensor(out=y[:, 2], in0=rest[:], in1=y[:, 1], op=ALU.subtract)
+
+        yw = y[:].bitcast(F32).rearrange("p l q c -> p c l q")
+        nc.vector.tensor_copy(out=words_b[:, :, 0:3, 4:6], in_=yw[:, :, :, 0:2])
+        nc.vector.tensor_copy(
+            out=words_b[:, :, 0:8, 7].rearrange("p c (k l) -> p c k l", k=2)[:, :, :, 1:4],
+            in_=yw[:, :, :, 6:10:3].rearrange("p c l k -> p c k l"),
+        )
+        nc.vector.tensor_copy(
+            out=words_a[:, :, 0:8, 0:3].rearrange("p c (k l) s -> p c k l s", k=2)[:, :, :, 0:3, :],
+            in_=yw[:, :, :, 0:6].rearrange("p c l (k s) -> p c k l s", k=2),
+        )
+        nc.vector.tensor_copy(out=words_a[:, :, 5:8, 3:6], in_=yw[:, :, :, 7:10])
+        nc.vector.tensor_copy(
+            out=words_a[:, :, 0:8, 6].rearrange("p c (k l) -> p c k l", k=2)[:, :, :, 1:4],
+            in_=yw[:, :, :, 2:6:3].rearrange("p c l k -> p c k l"),
+        )
+        nc.vector.tensor_copy(out=words_a[:, :, 1:4, 3], in_=yw[:, :, :, 6])
+
+        for g in range(2):
+            nc.scalar.copy(
+                out=scale_row[:, 512 * g : 512 * (g + 1)].rearrange("p (n t) -> p n t", t=4),
+                in_=scale_banks[g][:].rearrange("p t n -> p n t"),
+            )
+
+        q_grp = [keep.tile([P, 2, 256, 2], F32, name="q_grp%d" % d, align_bytes=64) for d in range(4)]
+        s_grp = [keep.tile([P, 2, 256, 2], F32, name="s_grp%d" % d, tag="s_grp%d" % d, align_bytes=64) for d in range(4)]
+        q_codes = [keep.tile([P, 2, 512], U32, name="q_codes%d" % h, align_bytes=64) for h in range(2)]
+        q_scales = [keep.tile([P, 2, 512], U8, name="q_scales%d" % h, align_bytes=64) for h in range(2)]
+        s_codes = [keep.tile([P, 2, w], U32, name="s_codes%d" % h, align_bytes=64) for h, w in enumerate((256, 512, 256))]
+        s_scales = [keep.tile([P, 2, w], U8, name="s_scales%d" % h, align_bytes=64) for h, w in enumerate((256, 512, 256))]
+        s_wide = [keep.tile([P, N], BF16, name="s_wide%d" % r) for r in range(8)]
+        held = {}
+
+        def widen(r, lo=0, hi=N):
+            nc.vector.tensor_tensor(out=s_wide[r][:, lo:hi], in0=s_raw[r // 2][:, r % 2, lo:hi].bitcast(FP8), in1=scale_row[:, lo:hi], op=ALU.mult)
+
+        def flip(kind, r, bk):
+            rows = q_raw[r // 2][:, r % 2, :] if kind == "q" else s_wide[r][:]
+            words = rows.bitcast(F32)
+            b = bank(bk, [P, 2, 2, P])
+            held[(kind, r)] = b
+            for g in range(2):
+                for u in range(2):
+                    nc.tensor.transpose(b[:, g, u, :], words[:, 256 * g + u : 256 * (g + 1) : 2], ident[:])
+
+        def group(kind, r, on_vector=False):
+            grp = (q_grp if kind == "q" else s_grp)[r // 2]
+            (nc.vector.tensor_copy if on_vector else nc.scalar.copy)(out=grp[:, :, P * (r % 2) : P * (r % 2 + 1), :], in_=held[(kind, r)][:].rearrange("p g u r -> p g r u"))
+
+        def quantise(kind, d, g):
+            grp, codes, scales = (q_grp, q_codes, q_scales) if kind == "q" else (s_grp, s_codes, s_scales)
+            h, lo = (d // 2, 256 * (d % 2)) if kind == "q" else ((d + 1) // 2, 256 * (d == 2))
+            cols = slice(lo, lo + 256)
+            nc.vector.quantize_mx(
+                out=codes[h][:, g, cols].bitcast(FP8X4),
+                scales=scales[h][:, g, cols],
+                in_=grp[d][:, g].rearrange("p r u -> p (r u)").bitcast(BF16),
+            )
+
+        total_bank = bank(3, [P, 1])
+        nc.tensor.matmul(total_bank[:], lhsT=ones[:], rhs=lam_sum[:], start=True, stop=True)
+        stoke(WARM[1])
+        flip("q", 0, 2)
+        group("q", 0)
+        stoke(WARM[2])
+        nc.vector.reciprocal(out=inv_total[:], in_=total_bank[:])
+
+        rows_a = keep.tile([P, 4, P], F32, name="rows_a")
+        rows_b = keep.tile([P, 4, P], F32, name="rows_b")
+
+        def table(words, rows, lo, hi, bk, on_vector):
+            b = bank(bk, [P, hi - lo, P])
+            for cp in range(lo, hi):
+                nc.tensor.transpose(b[:, cp - lo, :], words[:, cp].rearrange("p l s -> p (l s)"), ident[:])
+            if on_vector:
+                nc.vector.tensor_copy(out=rows[:, lo:hi], in_=b[:])
+            else:
+                nc.scalar.copy(out=rows[:, lo:hi], in_=b[:])
+
+        widen(0)
+        widen(1)
+        table(words_b, rows_b, 0, 2, 0, False)
+        table(words_a, rows_a, 0, 1, 4, False)
+        table(words_b, rows_b, 2, 4, 5, False)
+        table(words_a, rows_a, 1, 4, 6, False)
+
+        lam_bank = bank(7, [P, 4, P])
+        lam_words = lam_c[:].bitcast(F32)
+        lam_row = lam_bank[:].rearrange("p c n -> p (c n)").bitcast(BF16)
+
+        moving = rows_b[:].rearrange("p c n -> p (c n)").bitcast(BF16)
+        stationary = rows_a[:].bitcast(BF16)
+        sums = keep.tile([P, 8, 2], F32, name="sums")
+        tilted = keep.tile([P, 8], F32, name="tilted")
+
+        def pairs(c):
+            rec = ring.tile([P, N], F32, name="rec", bufs=4)
+            held[("rec", c)] = rec
+            for half in range(2):
+                b = bank((0, 1, 6)[(2 * c + half) % 3], [P, 512])
+                cols = slice(512 * half, 512 * (half + 1))
+                nc.tensor.matmul(b[:], lhsT=stationary[:, c // 2, c % 2 :: 2], rhs=moving[:, cols], start=True, stop=True)
+                nc.scalar.activation(
+                    out=rec[:, cols], in_=b[:], func=ACT.Abs_reciprocal_sqrt,
+                    scale=arg_scale[:, c : c + 1], bias=arg_bias[:, c : c + 1], accum_out=sums[:, c, half : half + 1],
+                )
+
+        def skew(c):
+            rec = held[("rec", c)]
+            nc.vector.scalar_tensor_tensor(
+                out=rec[:], in0=lam_row, scalar=lam32[:, c : c + 1], in1=rec[:],
+                op0=ALU.subtract, op1=ALU.mult, accum_out=tilted[:, c : c + 1],
+            )
+
+
+        def reorder_u(gx, tag):
+            uw = keep.tile([P, 2, N], U8, name="uw%d" % gx, tag=tag, align_bytes=64)
+            us = keep.tile([P, 2, 512], U8, name="us%d" % gx, align_bytes=64)
+            held[("uw", gx)] = uw
+            held[("us", gx)] = us
+            for g in range(2):
+                nc.gpsimd.tensor_copy(
+                    out=uw[:, g].rearrange("p (t m b) -> p t m b", t=4, b=2),
+                    in_=uw_raw[:, g, N * gx : N * (gx + 1)].rearrange("p (m t b) -> p t m b", t=4, b=2),
+                )
+            nc.gpsimd.tensor_copy(
+                out=us[:].rearrange("p g (t m) -> p g t m", t=4),
+                in_=us_raw[:, :, 512 * gx : 512 * (gx + 1)].rearrange("p g (m t) -> p g t m", t=4),
+            )
+
+        early_planes = keep.tile([P, 2, 4, 256], BF16, name="early_planes")
+        x_planes = keep.tile([P, 2, 4, 512], BF16, name="x_planes")
+        factor = keep.tile([P, 8], F32, name="factor")
+
+        def first_pass(dst, c, g, group_id, cols):
+            nc.tensor.matmul_mx(
+                dst, lhsT=held[("uw", c // 4)][:, g, 256 * (c % 4) : 256 * (c % 4 + 1)].bitcast(FP4X4),
+                lhsT_scale=held[("us", c // 4)][:, g, P * (c % 4) : P * (c % 4 + 1)],
+                rhs=s_codes[group_id][:, g, cols].bitcast(FP8X4), rhs_scale=s_scales[group_id][:, g, cols], start=(g == 0), stop=(g == 1),
+            )
+
+        def first_wide(c, bk):
+            b = bank(bk, [P, 512])
+            held[("y", c)] = b
+            for g in range(2):
+                first_pass(b[:], c, g, 1, slice(0, 512))
+
+        def first_narrow(r, gx, bk):
+            b = bank(bk, [P, 4, P])
+            held[("yn", r, gx)] = b
+            for t in range(4):
+                for g in range(2):
+                    first_pass(b[:, t, :], 4 * gx + t, g, 0 if r < 2 else 2, slice(P * (r % 2), P * (r % 2 + 1)))
+
+        def first_early(k, bk):
+            b = bank(bk, [P, 2, 256])
+            held[("ye", k)] = b
+            for j in range(2):
+                for a in range(2):
+                    for g in range(2):
+                        first_pass(b[:, j, P * a : P * (a + 1)], 2 * k + j, g, 0, slice(P * a, P * (a + 1)))
+
+        def shrink_early(k):
+            for j in range(2):
+                c = 2 * k + j
+                nc.scalar.activation(out=early_planes[:, c // 4, c % 4, :], in_=held[("ye", k)][:, j, :], func=ACT.Copy, scale=factor[:, c : c + 1])
+
+        def shrink_wide(c):
+            nc.scalar.activation(out=x_planes[:, c // 4, c % 4, :], in_=held[("y", c)][:], func=ACT.Copy, scale=factor[:, c : c + 1])
+
+        def x_group(r):
+            if ("xg", r) not in held:
+                held[("xg", r)] = ring.tile([P, 2, P, 4], BF16, name="xg", align_bytes=64)
+            return held[("xg", r)]
+
+        def shrink_narrow(r, gx):
+            nc.vector.tensor_tensor(
+                out=x_group(r)[:, gx],
+                in0=held[("yn", r, gx)][:].rearrange("p t n -> p n t"),
+                in1=factor[:, 4 * gx : 4 * gx + 4].unsqueeze(1).to_broadcast([P, P, 4]),
+                op=ALU.mult,
+            )
+
+        def weave(r):
+            nc.vector.tensor_copy(
+                out=x_group(r)[:].rearrange("p g (c i) t -> p g c t i", i=4),
+                in_=(early_planes[:, :, :, P * r : P * (r + 1)] if r < 2 else x_planes[:, :, :, P * (r - 2) : P * (r - 1)]).rearrange("p g t (c i) -> p g c t i", i=4),
+            )
+
+        def quantise_x(r):
+            xc = ring.tile([P, 2, P], U32, name="xc", align_bytes=64, bufs=4)
+            xs = ring.tile([P, 2, P], U8, name="xs", align_bytes=64, bufs=4)
+            held[("x", r)] = (xc, xs)
+            nc.vector.quantize_mx(
+                out=xc[:].rearrange("p g n -> p (g n)").bitcast(FP8X4),
+                scales=xs[:].rearrange("p g n -> p (g n)"),
+                in_=held[("xg", r)][:].rearrange("p g n t -> p (g n t)"),
+            )
+
+        out_rows = out.rearrange("(d p a) t -> d a p t", p=P, a=2)
+
+        def second(r, th, bk):
+            xc, xs = held[("x", r)]
+            b = bank(bk, [P, 512])
+            held[("o", r, th)] = b
+            for g in range(2):
+                nc.tensor.matmul_mx(
+                    b[:], lhsT=xc[:, g, :].bitcast(FP8X4), lhsT_scale=xs[:, g, :],
+                    rhs=q_codes[th][:, g, :].bitcast(FP8X4), rhs_scale=q_scales[th][:, g, :], start=(g == 0), stop=(g == 1),
+                )
+
+        def store(r, th, on_vector=False):
+            o = ring.tile([P, 512], F32, name="o", bufs=6)
+            if on_vector:
+                nc.vector.tensor_copy(out=o[:], in_=held[("o", r, th)][:])
+            else:
+                nc.scalar.copy(out=o[:], in_=held[("o", r, th)][:])
+            nc.sync.dma_start(out=out_rows[r // 2, r % 2, :, 512 * th : 512 * (th + 1)], in_=o[:])
+
+        both = keep.tile([P, 8], F32, name="both")
+        legs = keep.tile([P, 2, 8], F32, name="legs")
+        squares = keep.tile([P, 2, 8], F32, name="squares")
+        denom = keep.tile([P, 8], F32, name="denom")
+        inv_denom = keep.tile([P, 8], F32, name="inv_denom")
+        r_vals = keep.tile([P, 8], F32, name="r_vals")
+        r_sum = keep.tile([P, 1], F32, name="r_sum")
+        unscaled = keep.tile([P, 8], F32, name="unscaled")
+        pairs(0)
+        flip("s", 0, 2)
+        for cp in range(4):
+            nc.tensor.transpose(lam_bank[:, cp, :], lam_words[:, cp : cp + 1].to_broadcast([P, P]), ident[:])
+        flip("s", 1, 3)
+        group("s", 0, True)
+        group("s", 1, True)
+        quantise("s", 0, 0)
+        quantise("s", 0, 1)
+        reorder_u(0, "s_grp0")
+        reorder_u(1, "uw1")
+        for c in range(1, 8):
+            pairs(c)
+            skew(c - 1)
+            if c in (1, 3, 5, 6):
+                n = (1, 3, 5, 6).index(c)
+                flip("q", n + 1, (4, 5, 2, 3)[n])
+        nc.vector.tensor_tensor(out=both[:], in0=sums[:, :, 0], in1=sums[:, :, 1], op=ALU.add)
+        skew(7)
+        nc.vector.scalar_tensor_tensor(out=weight[:], in0=tilt_c[:], scalar=inv_total[:], in1=inv_lam[:], op0=ALU.mult, op1=ALU.mult)
+        flip("q", 5, 1)
+        group("q", 1)
+        first_early(0, 6)
+        group("q", 2)
+        flip("q", 6, 0)
+        group("q", 3)
+        first_early(1, 4)
+        group("q", 4)
+        flip("q", 7, 5)
+        group("q", 5)
+        group("q", 6)
+        nc.vector.tensor_tensor(out=legs[:, 1, :], in0=both[:], in1=h_lam[:], op=ALU.mult)
+        nc.vector.tensor_scalar(out=legs[:, 0, :], in0=tilted[:], scalar1=CONC - 1.0, scalar2=None, op0=ALU.add)
+        widen(2, 0, 512)
+        nc.vector.tensor_tensor(out=squares[:], in0=legs[:], in1=legs[:], op=ALU.mult)
+        widen(2, 512, N)
+        nc.vector.tensor_tensor(out=denom[:], in0=squares[:, 0, :], in1=squares[:, 1, :], op=ALU.add)
+        widen(3, 0, 256)
+        nc.vector.reciprocal(out=inv_denom[:], in_=denom[:])
+        widen(3, 256, 512)
+        nc.vector.scalar_tensor_tensor(out=r_vals[:], in0=inv_denom[:], scalar=1.0, in1=lam32[:], op0=ALU.mult, op1=ALU.mult, accum_out=r_sum[:])
+        nc.vector.tensor_tensor(out=unscaled[:], in0=denom[:], in1=weight[:], op=ALU.mult)
+        first_early(2, 2)
+        flip("s", 2, 3)
+        r_bank = bank(7, [P, 1])
+        nc.tensor.matmul(r_bank[:], lhsT=ones[:], rhs=r_sum[:], start=True, stop=True)
+        widen(3, 512, N)
+        nc.vector.tensor_scalar(out=factor[:], in0=unscaled[:], scalar1=r_bank[:], scalar2=None, op0=ALU.mult)
+        group("q", 7)
+        group("s", 2)
+        stoke(2, 1)
+        flip("s", 3, 5)
+        widen(4)
+        group("s", 3)
+        shrink_early(0)
+        flip("s", 4, 0)
+        first_early(3, 7)
+        widen(5)
+        quantise("s", 1, 0)
+        quantise("s", 1, 1)
+        group("s", 4)
+        shrink_early(1)
+        flip("s", 5, 1)
+        stoke(1, 3)
+        group("s", 5)
+        quantise("q", 0, 0)
+        quantise("q", 0, 1)
+        quantise("s", 2, 0)
+        quantise("s", 2, 1)
+        shrink_early(2)
+        shrink_early(3)
+        quantise("q", 1, 0)
+        quantise("q", 1, 1)
+        weave(0)
+        quantise("q", 2, 0)
+        quantise_x(0)
+        weave(1)
+        quantise("q", 2, 1)
+        quantise_x(1)
+        wide_banks = (3, 5, 6, 0, 4, 1, 2, 7)
+        for c in range(4):
+            first_wide(c, wide_banks[c])
+            shrink_wide(c)
+        widen(6)
+        widen(7)
+        second(0, 0, 3)
+        for c in range(4, 6):
+            first_wide(c, wide_banks[c])
+            shrink_wide(c)
+        second(1, 0, 5)
+        for c in range(6, 8):
+            first_wide(c, wide_banks[c])
+            shrink_wide(c)
+        quantise("q", 3, 0)
+        quantise("q", 3, 1)
+        flip("s", 6, 6)
+        flip("s", 7, 0)
+        weave(2)
+        store(0, 0, True)
+        group("s", 6)
+        group("s", 7)
+        second(0, 1, 4)
+        second(1, 1, 1)
+        quantise_x(2)
+        weave(3)
+        store(1, 0)
+        quantise("s", 3, 0)
+        quantise("s", 3, 1)
+        second(2, 0, 2)
+        store(0, 1)
+        second(2, 1, 7)
+        store(1, 1)
+        quantise_x(3)
+        weave(4)
+        first_narrow(6, 0, 3)
+        first_narrow(6, 1, 6)
+        store(2, 0)
+        store(2, 1)
+        second(3, 0, 0)
+        second(3, 1, 5)
+        quantise_x(4)
+        weave(5)
+        first_narrow(7, 0, 4)
+        first_narrow(7, 1, 1)
+        store(3, 0)
+        store(3, 1)
+        second(4, 0, 2)
+        second(4, 1, 7)
+        quantise_x(5)
+        shrink_narrow(6, 0)
+        shrink_narrow(6, 1)
+        store(4, 0)
+        store(4, 1)
+        second(5, 0, 0)
+        second(5, 1, 5)
+        shrink_narrow(7, 0)
+        quantise_x(6)
+        shrink_narrow(7, 1)
+        store(5, 0)
+        store(5, 1)
+        second(6, 0, 2)
+        second(6, 1, 7)
+        quantise_x(7)
+        store(6, 0)
+        second(7, 0, 3)
+        second(7, 1, 6)
+        store(6, 1, True)
+        store(7, 0)
+        store(7, 1, True)

@@ -18,7 +18,7 @@ P = 128
 N = 1024
 CONC = 0.25
 H = (CONC**2) ** 0.35 * float(N) ** (-0.35)
-WARM = (5, 2, 1)
+WARM = (4, 2, 2)
 FLOPS = 2 * 2 * N * N * N
 
 
@@ -37,7 +37,7 @@ def tile_quadraticinverseshrinkagesignalpnl_w4_kernel(
 
         lam_c = keep.tile([P, 8], BF16, name="lam_c")
         scale_c = keep.tile([P, 8], F32, name="scale_c")
-        tilt_c = keep.tile([P, 8], BF16, name="tilt_c")
+        tilt_c = keep.tile([P, 8], BF16, name="tilt_c", tag="uw0", align_bytes=64)
         q_raw = [keep.tile([P, 2, N], BF16, name="q_raw%d" % d) for d in range(4)]
         s_raw = [keep.tile([P, 2, N], U8, name="s_raw%d" % d) for d in range(4)]
         uw_raw = keep.tile([P, 2, 2 * N], U8, name="uw_raw")
@@ -48,7 +48,7 @@ def tile_quadraticinverseshrinkagesignalpnl_w4_kernel(
         nc.gpsimd.memset(ones[:], 1.0)
         make_identity(nc, ident[:])
 
-        def stoke(count, bk=7):
+        def stoke(count, bk=6):
             b = bank(bk, [P, P])
             for n in range(count):
                 nc.tensor.matmul(b[:], lhsT=ones[:], rhs=ones[:], start=True, stop=True)
@@ -66,6 +66,7 @@ def tile_quadraticinverseshrinkagesignalpnl_w4_kernel(
         load_q(0)
         load_s(0)
         nc.sync.dma_start(out=tilt_c[:].rearrange("p (g t) -> p g t", g=2), in_=tilt.rearrange("(g p t) -> p g t", g=2, t=4))
+        load_s(1)
         load_q(1)
         load_q(2)
 
@@ -94,7 +95,6 @@ def tile_quadraticinverseshrinkagesignalpnl_w4_kernel(
                 out=us_raw[32 * quad : 32 * quad + 4].bitcast(I32),
                 in_=u_scales[:, 4 * quad : 4 * quad + 4, :].rearrange("g r n -> r g n").bitcast(I32),
             )
-        load_s(1)
         load_s(2)
         load_q(3)
         load_s(3)
@@ -192,8 +192,8 @@ def tile_quadraticinverseshrinkagesignalpnl_w4_kernel(
         s_grp = [keep.tile([P, 2, 256, 2], F32, name="s_grp%d" % d, tag="s_grp%d" % d, align_bytes=64) for d in range(4)]
         q_codes = [keep.tile([P, 2, 512], U32, name="q_codes%d" % h, align_bytes=64) for h in range(2)]
         q_scales = [keep.tile([P, 2, 512], U8, name="q_scales%d" % h, align_bytes=64) for h in range(2)]
-        s_codes = [keep.tile([P, 2, w], U32, name="s_codes%d" % h, align_bytes=64) for h, w in enumerate((256, 512, 256))]
-        s_scales = [keep.tile([P, 2, w], U8, name="s_scales%d" % h, align_bytes=64) for h, w in enumerate((256, 512, 256))]
+        s_codes = [keep.tile([P, 2, w], U32, name="s_codes%d" % h, align_bytes=64) for h, w in enumerate((512, 512))]
+        s_scales = [keep.tile([P, 2, w], U8, name="s_scales%d" % h, align_bytes=64) for h, w in enumerate((512, 512))]
         s_wide = [keep.tile([P, N], BF16, name="s_wide%d" % r) for r in range(8)]
         held = {}
 
@@ -215,7 +215,7 @@ def tile_quadraticinverseshrinkagesignalpnl_w4_kernel(
 
         def quantise(kind, d, g):
             grp, codes, scales = (q_grp, q_codes, q_scales) if kind == "q" else (s_grp, s_codes, s_scales)
-            h, lo = (d // 2, 256 * (d % 2)) if kind == "q" else ((d + 1) // 2, 256 * (d == 2))
+            h, lo = d // 2, 256 * (d % 2)
             cols = slice(lo, lo + 256)
             nc.vector.quantize_mx(
                 out=codes[h][:, g, cols].bitcast(FP8X4),
@@ -223,13 +223,13 @@ def tile_quadraticinverseshrinkagesignalpnl_w4_kernel(
                 in_=grp[d][:, g].rearrange("p r u -> p (r u)").bitcast(BF16),
             )
 
-        total_bank = bank(3, [P, 1])
-        nc.tensor.matmul(total_bank[:], lhsT=ones[:], rhs=lam_sum[:], start=True, stop=True)
+        lam_bank = bank(7, [P, 4, P])
+        lam_words = lam_c[:].bitcast(F32)
+        lam_row = lam_bank[:].rearrange("p c n -> p (c n)").bitcast(BF16)
         stoke(WARM[1])
         flip("q", 0, 2)
-        group("q", 0)
         stoke(WARM[2])
-        nc.vector.reciprocal(out=inv_total[:], in_=total_bank[:])
+        group("q", 0)
 
         rows_a = keep.tile([P, 4, P], F32, name="rows_a")
         rows_b = keep.tile([P, 4, P], F32, name="rows_b")
@@ -245,31 +245,35 @@ def tile_quadraticinverseshrinkagesignalpnl_w4_kernel(
 
         widen(0)
         widen(1)
+        widen(2)
         table(words_b, rows_b, 0, 2, 0, False)
         table(words_a, rows_a, 0, 1, 4, False)
         table(words_b, rows_b, 2, 4, 5, False)
         table(words_a, rows_a, 1, 4, 6, False)
-
-        lam_bank = bank(7, [P, 4, P])
-        lam_words = lam_c[:].bitcast(F32)
-        lam_row = lam_bank[:].rearrange("p c n -> p (c n)").bitcast(BF16)
+        for cp in range(4):
+            nc.tensor.transpose(lam_bank[:, cp, :], lam_words[:, cp : cp + 1].to_broadcast([P, P]), ident[:])
+        total_bank = bank(3, [P, 1])
+        nc.tensor.matmul(total_bank[:], lhsT=ones[:], rhs=lam_sum[:], start=True, stop=True)
+        nc.vector.reciprocal(out=inv_total[:], in_=total_bank[:])
+        widen(3)
+        nc.vector.scalar_tensor_tensor(out=weight[:], in0=tilt_c[:], scalar=inv_total[:], in1=inv_lam[:], op0=ALU.mult, op1=ALU.mult)
 
         moving = rows_b[:].rearrange("p c n -> p (c n)").bitcast(BF16)
         stationary = rows_a[:].bitcast(BF16)
         sums = keep.tile([P, 8, 2], F32, name="sums")
         tilted = keep.tile([P, 8], F32, name="tilted")
 
-        def pairs(c):
-            rec = ring.tile([P, N], F32, name="rec", bufs=4)
-            held[("rec", c)] = rec
-            for half in range(2):
-                b = bank((0, 1, 6)[(2 * c + half) % 3], [P, 512])
-                cols = slice(512 * half, 512 * (half + 1))
-                nc.tensor.matmul(b[:], lhsT=stationary[:, c // 2, c % 2 :: 2], rhs=moving[:, cols], start=True, stop=True)
-                nc.scalar.activation(
-                    out=rec[:, cols], in_=b[:], func=ACT.Abs_reciprocal_sqrt,
-                    scale=arg_scale[:, c : c + 1], bias=arg_bias[:, c : c + 1], accum_out=sums[:, c, half : half + 1],
-                )
+        def pairs(c, half):
+            if half == 0:
+                held[("rec", c)] = ring.tile([P, N], F32, name="rec", bufs=4)
+            rec = held[("rec", c)]
+            b = bank((0, 1, 6)[(2 * c + half) % 3], [P, 512])
+            cols = slice(512 * half, 512 * (half + 1))
+            nc.tensor.matmul(b[:], lhsT=stationary[:, c // 2, c % 2 :: 2], rhs=moving[:, cols], start=True, stop=True)
+            nc.scalar.activation(
+                out=rec[:, cols], in_=b[:], func=ACT.Abs_reciprocal_sqrt,
+                scale=arg_scale[:, c : c + 1], bias=arg_bias[:, c : c + 1], accum_out=sums[:, c, half : half + 1],
+            )
 
         def skew(c):
             rec = held[("rec", c)]
@@ -281,81 +285,51 @@ def tile_quadraticinverseshrinkagesignalpnl_w4_kernel(
 
         def reorder_u(gx, tag):
             uw = keep.tile([P, 2, N], U8, name="uw%d" % gx, tag=tag, align_bytes=64)
-            us = keep.tile([P, 2, 512], U8, name="us%d" % gx, align_bytes=64)
             held[("uw", gx)] = uw
-            held[("us", gx)] = us
-            for g in range(2):
-                nc.gpsimd.tensor_copy(
-                    out=uw[:, g].rearrange("p (t m b) -> p t m b", t=4, b=2),
-                    in_=uw_raw[:, g, N * gx : N * (gx + 1)].rearrange("p (m t b) -> p t m b", t=4, b=2),
-                )
             nc.gpsimd.tensor_copy(
-                out=us[:].rearrange("p g (t m) -> p g t m", t=4),
+                out=uw[:].rearrange("p g (t m b) -> p g t m b", t=4, b=2),
+                in_=uw_raw[:, :, N * gx : N * (gx + 1)].rearrange("p g (m t b) -> p g t m b", t=4, b=2),
+            )
+
+        def reorder_scales(gx, tag):
+            held[("us", gx)] = keep.tile([P, 2, 512], U8, name="us%d" % gx, tag=tag, align_bytes=64)
+            nc.gpsimd.tensor_copy(
+                out=held[("us", gx)][:].rearrange("p g (t m) -> p g t m", t=4),
                 in_=us_raw[:, :, 512 * gx : 512 * (gx + 1)].rearrange("p g (m t) -> p g t m", t=4),
             )
 
-        early_planes = keep.tile([P, 2, 4, 256], BF16, name="early_planes")
-        x_planes = keep.tile([P, 2, 4, 512], BF16, name="x_planes")
+        x_planes = [keep.tile([P, 2, 4, 512], BF16, name="x_planes%d" % h) for h in range(2)]
         factor = keep.tile([P, 8], F32, name="factor")
 
-        def first_pass(dst, c, g, group_id, cols):
-            nc.tensor.matmul_mx(
-                dst, lhsT=held[("uw", c // 4)][:, g, 256 * (c % 4) : 256 * (c % 4 + 1)].bitcast(FP4X4),
-                lhsT_scale=held[("us", c // 4)][:, g, P * (c % 4) : P * (c % 4 + 1)],
-                rhs=s_codes[group_id][:, g, cols].bitcast(FP8X4), rhs_scale=s_scales[group_id][:, g, cols], start=(g == 0), stop=(g == 1),
-            )
+        def first(h, c, bk, passes=(0, 1)):
+            if 0 in passes:
+                held[("y", h, c)] = bank(bk, [P, 512])
+            b = held[("y", h, c)]
+            for g in passes:
+                nc.tensor.matmul_mx(
+                    b[:],
+                    lhsT=held[("uw", c // 4)][:, g, 256 * (c % 4) : 256 * (c % 4 + 1)].bitcast(FP4X4),
+                    lhsT_scale=held[("us", c // 4)][:, g, P * (c % 4) : P * (c % 4 + 1)],
+                    rhs=s_codes[h][:, g, :].bitcast(FP8X4), rhs_scale=s_scales[h][:, g, :], start=(g == 0), stop=(g == 1),
+                )
 
-        def first_wide(c, bk):
-            b = bank(bk, [P, 512])
-            held[("y", c)] = b
-            for g in range(2):
-                first_pass(b[:], c, g, 1, slice(0, 512))
-
-        def first_narrow(r, gx, bk):
-            b = bank(bk, [P, 4, P])
-            held[("yn", r, gx)] = b
-            for t in range(4):
-                for g in range(2):
-                    first_pass(b[:, t, :], 4 * gx + t, g, 0 if r < 2 else 2, slice(P * (r % 2), P * (r % 2 + 1)))
-
-        def first_early(k, bk):
-            b = bank(bk, [P, 2, 256])
-            held[("ye", k)] = b
-            for j in range(2):
-                for a in range(2):
-                    for g in range(2):
-                        first_pass(b[:, j, P * a : P * (a + 1)], 2 * k + j, g, 0, slice(P * a, P * (a + 1)))
-
-        def shrink_early(k):
-            for j in range(2):
-                c = 2 * k + j
-                nc.scalar.activation(out=early_planes[:, c // 4, c % 4, :], in_=held[("ye", k)][:, j, :], func=ACT.Copy, scale=factor[:, c : c + 1])
-
-        def shrink_wide(c):
-            nc.scalar.activation(out=x_planes[:, c // 4, c % 4, :], in_=held[("y", c)][:], func=ACT.Copy, scale=factor[:, c : c + 1])
-
-        def x_group(r):
-            if ("xg", r) not in held:
-                held[("xg", r)] = ring.tile([P, 2, P, 4], BF16, name="xg", align_bytes=64)
-            return held[("xg", r)]
-
-        def shrink_narrow(r, gx):
-            nc.vector.tensor_tensor(
-                out=x_group(r)[:, gx],
-                in0=held[("yn", r, gx)][:].rearrange("p t n -> p n t"),
-                in1=factor[:, 4 * gx : 4 * gx + 4].unsqueeze(1).to_broadcast([P, P, 4]),
-                op=ALU.mult,
-            )
+        def shrink(h, c, on_vector=False):
+            if on_vector:
+                nc.vector.tensor_scalar(out=x_planes[h][:, c // 4, c % 4, :], in0=held[("y", h, c)][:], scalar1=factor[:, c : c + 1], scalar2=None, op0=ALU.mult)
+            else:
+                nc.scalar.activation(out=x_planes[h][:, c // 4, c % 4, :], in_=held[("y", h, c)][:], func=ACT.Copy, scale=factor[:, c : c + 1])
 
         def weave(r):
+            xg = ring.tile([P, 2, P, 4], BF16, name="xg", align_bytes=64)
+            held[("xg", r)] = xg
             nc.vector.tensor_copy(
-                out=x_group(r)[:].rearrange("p g (c i) t -> p g c t i", i=4),
-                in_=(early_planes[:, :, :, P * r : P * (r + 1)] if r < 2 else x_planes[:, :, :, P * (r - 2) : P * (r - 1)]).rearrange("p g t (c i) -> p g c t i", i=4),
+                out=xg[:].rearrange("p g (c i) t -> p g c t i", i=4),
+                in_=x_planes[r // 4][:, :, :, P * (r % 4) : P * (r % 4 + 1)].rearrange("p g t (c i) -> p g c t i", i=4),
             )
 
         def quantise_x(r):
-            xc = ring.tile([P, 2, P], U32, name="xc", align_bytes=64, bufs=4)
-            xs = ring.tile([P, 2, P], U8, name="xs", align_bytes=64, bufs=4)
+            xc = ring.tile([P, 2, P], U32, name="xc", align_bytes=64, bufs=8)
+            xs = ring.tile([P, 2, P], U8, name="xs", align_bytes=64, bufs=8)
             held[("x", r)] = (xc, xs)
             nc.vector.quantize_mx(
                 out=xc[:].rearrange("p g n -> p (g n)").bitcast(FP8X4),
@@ -365,23 +339,24 @@ def tile_quadraticinverseshrinkagesignalpnl_w4_kernel(
 
         out_rows = out.rearrange("(d p a) t -> d a p t", p=P, a=2)
 
-        def second(r, th, bk):
+        def second(r, lo, width, bk):
             xc, xs = held[("x", r)]
-            b = bank(bk, [P, 512])
-            held[("o", r, th)] = b
+            b = bank(bk, [P, width])
+            held[("o", r, lo)] = b
+            cols = slice(lo % 512, lo % 512 + width)
             for g in range(2):
                 nc.tensor.matmul_mx(
                     b[:], lhsT=xc[:, g, :].bitcast(FP8X4), lhsT_scale=xs[:, g, :],
-                    rhs=q_codes[th][:, g, :].bitcast(FP8X4), rhs_scale=q_scales[th][:, g, :], start=(g == 0), stop=(g == 1),
+                    rhs=q_codes[lo // 512][:, g, cols].bitcast(FP8X4), rhs_scale=q_scales[lo // 512][:, g, cols], start=(g == 0), stop=(g == 1),
                 )
 
-        def store(r, th, on_vector=False):
-            o = ring.tile([P, 512], F32, name="o", bufs=6)
-            if on_vector:
-                nc.vector.tensor_copy(out=o[:], in_=held[("o", r, th)][:])
-            else:
-                nc.scalar.copy(out=o[:], in_=held[("o", r, th)][:])
-            nc.sync.dma_start(out=out_rows[r // 2, r % 2, :, 512 * th : 512 * (th + 1)], in_=o[:])
+        def empty(r, lo, width, on_vector=False):
+            if lo == 0:
+                held[("out", r)] = ring.tile([P, N], F32, name="o", bufs=4)
+            (nc.vector.tensor_copy if on_vector else nc.scalar.copy)(out=held[("out", r)][:, lo : lo + width], in_=held[("o", r, lo)][:])
+
+        def store(r, lo, width):
+            nc.sync.dma_start(out=out_rows[r // 2, r % 2, :, lo : lo + width], in_=held[("out", r)][:, lo : lo + width])
 
         both = keep.tile([P, 8], F32, name="both")
         legs = keep.tile([P, 2, 8], F32, name="legs")
@@ -391,152 +366,139 @@ def tile_quadraticinverseshrinkagesignalpnl_w4_kernel(
         r_vals = keep.tile([P, 8], F32, name="r_vals")
         r_sum = keep.tile([P, 1], F32, name="r_sum")
         unscaled = keep.tile([P, 8], F32, name="unscaled")
-        pairs(0)
-        flip("s", 0, 2)
-        for cp in range(4):
-            nc.tensor.transpose(lam_bank[:, cp, :], lam_words[:, cp : cp + 1].to_broadcast([P, P]), ident[:])
-        flip("s", 1, 3)
-        group("s", 0, True)
-        group("s", 1, True)
-        quantise("s", 0, 0)
-        quantise("s", 0, 1)
-        reorder_u(0, "s_grp0")
+
+        reorder_u(0, "uw0")
+        reorder_scales(0, "us0")
         reorder_u(1, "uw1")
-        for c in range(1, 8):
-            pairs(c)
-            skew(c - 1)
-            if c in (1, 3, 5, 6):
-                n = (1, 3, 5, 6).index(c)
-                flip("q", n + 1, (4, 5, 2, 3)[n])
-        nc.vector.tensor_tensor(out=both[:], in0=sums[:, :, 0], in1=sums[:, :, 1], op=ALU.add)
+        for c in range(8):
+            pairs(c, 0)
+            pairs(c, 1)
+            if 2 <= c < 6:
+                group("s", c - 2, c == 2)
+            flip(*(("s", c) if c < 4 else ("q", c - 3)), 2 + c % 4)
+            if c >= 1:
+                skew(c - 1)
+            if c == 6:
+                for g in range(2):
+                    for d in range(2):
+                        quantise("s", d, g)
+                reorder_scales(1, "s_grp1")
         skew(7)
-        nc.vector.scalar_tensor_tensor(out=weight[:], in0=tilt_c[:], scalar=inv_total[:], in1=inv_lam[:], op0=ALU.mult, op1=ALU.mult)
-        flip("q", 5, 1)
+        for g in range(2):
+            for c in range(3):
+                first(0, c, (1, 6, 0)[c], (g,))
         group("q", 1)
-        first_early(0, 6)
+        flip("q", 5, 2)
         group("q", 2)
-        flip("q", 6, 0)
+        first(0, 3, 3)
         group("q", 3)
-        first_early(1, 4)
+        flip("q", 6, 4)
         group("q", 4)
-        flip("q", 7, 5)
         group("q", 5)
         group("q", 6)
-        nc.vector.tensor_tensor(out=legs[:, 1, :], in0=both[:], in1=h_lam[:], op=ALU.mult)
+        nc.vector.tensor_tensor(out=both[:], in0=sums[:, :, 0], in1=sums[:, :, 1], op=ALU.add)
         nc.vector.tensor_scalar(out=legs[:, 0, :], in0=tilted[:], scalar1=CONC - 1.0, scalar2=None, op0=ALU.add)
-        widen(2, 0, 512)
+        widen(4, 0, 256)
+        nc.vector.tensor_tensor(out=legs[:, 1, :], in0=both[:], in1=h_lam[:], op=ALU.mult)
+        widen(4, 256, 512)
         nc.vector.tensor_tensor(out=squares[:], in0=legs[:], in1=legs[:], op=ALU.mult)
-        widen(2, 512, N)
+        widen(4, 512, 768)
         nc.vector.tensor_tensor(out=denom[:], in0=squares[:, 0, :], in1=squares[:, 1, :], op=ALU.add)
-        widen(3, 0, 256)
+        widen(4, 768, N)
         nc.vector.reciprocal(out=inv_denom[:], in_=denom[:])
-        widen(3, 256, 512)
+        widen(5, 0, 256)
         nc.vector.scalar_tensor_tensor(out=r_vals[:], in0=inv_denom[:], scalar=1.0, in1=lam32[:], op0=ALU.mult, op1=ALU.mult, accum_out=r_sum[:])
         nc.vector.tensor_tensor(out=unscaled[:], in0=denom[:], in1=weight[:], op=ALU.mult)
-        first_early(2, 2)
-        flip("s", 2, 3)
+        first(0, 4, 5)
         r_bank = bank(7, [P, 1])
         nc.tensor.matmul(r_bank[:], lhsT=ones[:], rhs=r_sum[:], start=True, stop=True)
-        widen(3, 512, N)
+        widen(5, 256, N)
         nc.vector.tensor_scalar(out=factor[:], in0=unscaled[:], scalar1=r_bank[:], scalar2=None, op0=ALU.mult)
-        group("q", 7)
-        group("s", 2)
-        stoke(2, 1)
-        flip("s", 3, 5)
-        widen(4)
-        group("s", 3)
-        shrink_early(0)
-        flip("s", 4, 0)
-        first_early(3, 7)
-        widen(5)
-        quantise("s", 1, 0)
-        quantise("s", 1, 1)
+        widen(6)
+        widen(7)
+        first(0, 5, 4)
+        flip("s", 4, 2)
+        flip("s", 5, 7)
+        shrink(0, 0)
+        shrink(0, 1)
         group("s", 4)
-        shrink_early(1)
-        flip("s", 5, 1)
-        stoke(1, 3)
         group("s", 5)
-        quantise("q", 0, 0)
-        quantise("q", 0, 1)
+        first(0, 6, 1)
+        flip("s", 6, 6)
+        flip("s", 7, 2)
+        shrink(0, 2)
+        group("s", 6)
+        group("s", 7)
+        first(0, 7, 7)
+        flip("q", 7, 0)
         quantise("s", 2, 0)
         quantise("s", 2, 1)
-        shrink_early(2)
-        shrink_early(3)
-        quantise("q", 1, 0)
-        quantise("q", 1, 1)
+        shrink(0, 3, True)
+        shrink(0, 4, True)
+        quantise("s", 3, 0)
+        quantise("s", 3, 1)
+        for c in range(5, 8):
+            shrink(0, c)
+        group("q", 7)
+        for d in range(2):
+            for g in range(2):
+                quantise("q", d, g)
         weave(0)
         quantise("q", 2, 0)
         quantise_x(0)
-        weave(1)
         quantise("q", 2, 1)
-        quantise_x(1)
-        wide_banks = (3, 5, 6, 0, 4, 1, 2, 7)
-        for c in range(4):
-            first_wide(c, wide_banks[c])
-            shrink_wide(c)
-        widen(6)
-        widen(7)
-        second(0, 0, 3)
-        for c in range(4, 6):
-            first_wide(c, wide_banks[c])
-            shrink_wide(c)
-        second(1, 0, 5)
-        for c in range(6, 8):
-            first_wide(c, wide_banks[c])
-            shrink_wide(c)
         quantise("q", 3, 0)
         quantise("q", 3, 1)
-        flip("s", 6, 6)
-        flip("s", 7, 0)
+        weave(1)
+        for g in range(2):
+            for c in range(2):
+                first(1, c, (3, 6)[c], (g,))
+        for c in range(2, 5):
+            first(1, c, (2, 5, 4)[c - 2])
+        for c in range(3):
+            shrink(1, c)
+        second(0, 0, 512, 1)
+        first(1, 5, 7)
+        second(0, 512, 512, 0)
+        quantise_x(1)
         weave(2)
-        store(0, 0, True)
-        group("s", 6)
-        group("s", 7)
-        second(0, 1, 4)
-        second(1, 1, 1)
+        empty(0, 0, 512)
+        store(0, 0, 512)
+        shrink(1, 3)
+        empty(0, 512, 512)
+        store(0, 512, 512)
+        first(1, 6, 3)
+        first(1, 7, 6)
         quantise_x(2)
+        shrink(1, 4, True)
+        second(1, 0, 512, 2)
+        second(1, 512, 512, 5)
+        shrink(1, 5)
         weave(3)
-        store(1, 0)
-        quantise("s", 3, 0)
-        quantise("s", 3, 1)
-        second(2, 0, 2)
-        store(0, 1)
-        second(2, 1, 7)
-        store(1, 1)
+        shrink(1, 6)
+        shrink(1, 7, True)
+        for th in range(2):
+            empty(1, 512 * th, 512)
+            store(1, 512 * th, 512)
         quantise_x(3)
+        rotation = (1, 0, 4, 7, 3, 6, 2, 5)
         weave(4)
-        first_narrow(6, 0, 3)
-        first_narrow(6, 1, 6)
-        store(2, 0)
-        store(2, 1)
-        second(3, 0, 0)
-        second(3, 1, 5)
-        quantise_x(4)
-        weave(5)
-        first_narrow(7, 0, 4)
-        first_narrow(7, 1, 1)
-        store(3, 0)
-        store(3, 1)
-        second(4, 0, 2)
-        second(4, 1, 7)
-        quantise_x(5)
-        shrink_narrow(6, 0)
-        shrink_narrow(6, 1)
-        store(4, 0)
-        store(4, 1)
-        second(5, 0, 0)
-        second(5, 1, 5)
-        shrink_narrow(7, 0)
-        quantise_x(6)
-        shrink_narrow(7, 1)
-        store(5, 0)
-        store(5, 1)
-        second(6, 0, 2)
-        second(6, 1, 7)
-        quantise_x(7)
-        store(6, 0)
-        second(7, 0, 3)
-        second(7, 1, 6)
-        store(6, 1, True)
-        store(7, 0)
-        store(7, 1, True)
+        for r in range(2, 7):
+            for th in range(2):
+                second(r, 512 * th, 512, rotation[(2 * r - 4 + th) % 8])
+            if r + 2 < 8:
+                quantise_x(r + 2)
+            if r + 3 < 8:
+                weave(r + 3)
+            for th in range(2):
+                empty(r, 512 * th, 512, r >= 5 and th == 1)
+                store(r, 512 * th, 512)
+        second(7, 0, 512, 4)
+        second(7, 512, 256, 7)
+        second(7, 768, 256, 3)
+        empty(7, 0, 512)
+        store(7, 0, 512)
+        empty(7, 512, 256, True)
+        store(7, 512, 256)
+        empty(7, 768, 256)
+        store(7, 768, 256)

@@ -62,7 +62,7 @@ def tile_quadraticinverseshrinkagesignalpnl_w4_kernel(
             nc.sync.dma_start(out=s_raw[d][:], in_=signals_bytes[256 * d : 256 * (d + 1), :].rearrange("(p a) k -> p a k", a=2))
 
         nc.sync.dma_start(out=lam_c[:].rearrange("p (g t) -> p g t", g=2), in_=lam.rearrange("(g p t) -> p g t", g=2, t=4))
-        nc.sync.dma_start(out=scale_c[:].rearrange("p (g t) -> p g t", g=2), in_=signals_scale.rearrange("o (g p t) -> p (o g) t", g=2, t=4))
+        nc.scalar.dma_start(out=scale_c[:].rearrange("p (g t) -> p g t", g=2), in_=signals_scale.rearrange("o (g p t) -> p (o g) t", g=2, t=4))
         load_q(0)
         load_s(0)
         nc.sync.dma_start(out=tilt_c[:].rearrange("p (g t) -> p g t", g=2), in_=tilt.rearrange("(g p t) -> p g t", g=2, t=4))
@@ -319,34 +319,31 @@ def tile_quadraticinverseshrinkagesignalpnl_w4_kernel(
             else:
                 nc.scalar.activation(out=x_planes[h][:, c // 4, c % 4, :], in_=held[("y", h, c)][:], func=ACT.Copy, scale=factor[:, c : c + 1])
 
-        def weave(r):
-            xg = ring.tile([P, 2, P, 4], BF16, name="xg", align_bytes=64)
-            held[("xg", r)] = xg
-            nc.vector.tensor_copy(
-                out=xg[:].rearrange("p g (c i) t -> p g c t i", i=4),
-                in_=x_planes[r // 4][:, :, :, P * (r % 4) : P * (r % 4 + 1)].rearrange("p g t (c i) -> p g c t i", i=4),
-            )
+        x_codes = [keep.tile([P, 2, 256], U32, name="x_codes%d" % d, align_bytes=64) for d in range(4)]
+        x_scales = [keep.tile([P, 2, 256], U8, name="x_scales%d" % d, align_bytes=64) for d in range(4)]
 
-        def quantise_x(r):
-            xc = ring.tile([P, 2, P], U32, name="xc", align_bytes=64, bufs=8)
-            xs = ring.tile([P, 2, P], U8, name="xs", align_bytes=64, bufs=8)
-            held[("x", r)] = (xc, xs)
+        def weave(d, gx):
+            xg = ring.tile([P, 256, 4], BF16, name="xg", align_bytes=64)
+            held[("xg", d, gx)] = xg
+            nc.vector.tensor_copy(out=xg[:], in_=x_planes[d // 2][:, gx, :, 256 * (d % 2) : 256 * (d % 2 + 1)].rearrange("p t n -> p n t"))
+
+        def quantise_x(d, gx):
             nc.vector.quantize_mx(
-                out=xc[:].rearrange("p g n -> p (g n)").bitcast(FP8X4),
-                scales=xs[:].rearrange("p g n -> p (g n)"),
-                in_=held[("xg", r)][:].rearrange("p g n t -> p (g n t)"),
+                out=x_codes[d][:, gx, :].bitcast(FP8X4),
+                scales=x_scales[d][:, gx, :],
+                in_=held[("xg", d, gx)][:].rearrange("p n t -> p (n t)"),
             )
 
         out_rows = out.rearrange("(d p a) t -> d a p t", p=P, a=2)
 
         def second(r, lo, width, bk):
-            xc, xs = held[("x", r)]
+            tokens = slice(P * (r % 2), P * (r % 2 + 1))
             b = bank(bk, [P, width])
             held[("o", r, lo)] = b
             cols = slice(lo % 512, lo % 512 + width)
             for g in range(2):
                 nc.tensor.matmul_mx(
-                    b[:], lhsT=xc[:, g, :].bitcast(FP8X4), lhsT_scale=xs[:, g, :],
+                    b[:], lhsT=x_codes[r // 2][:, g, tokens].bitcast(FP8X4), lhsT_scale=x_scales[r // 2][:, g, tokens],
                     rhs=q_codes[lo // 512][:, g, cols].bitcast(FP8X4), rhs_scale=q_scales[lo // 512][:, g, cols], start=(g == 0), stop=(g == 1),
                 )
 
@@ -431,6 +428,8 @@ def tile_quadraticinverseshrinkagesignalpnl_w4_kernel(
         group("s", 7)
         first(0, 7, 7)
         flip("q", 7, 0)
+        quantise("q", 0, 0)
+        quantise("q", 0, 1)
         quantise("s", 2, 0)
         quantise("s", 2, 1)
         shrink(0, 3, True)
@@ -440,65 +439,67 @@ def tile_quadraticinverseshrinkagesignalpnl_w4_kernel(
         for c in range(5, 8):
             shrink(0, c)
         group("q", 7)
-        for d in range(2):
+        weave(0, 0)
+        quantise("q", 1, 0)
+        weave(0, 1)
+        quantise_x(0, 0)
+        quantise("q", 1, 1)
+        quantise_x(0, 1)
+        for d in range(2, 4):
             for g in range(2):
                 quantise("q", d, g)
-        weave(0)
-        quantise("q", 2, 0)
-        quantise_x(0)
-        quantise("q", 2, 1)
-        quantise("q", 3, 0)
-        quantise("q", 3, 1)
-        weave(1)
         for g in range(2):
             for c in range(2):
                 first(1, c, (3, 6)[c], (g,))
         for c in range(2, 5):
             first(1, c, (2, 5, 4)[c - 2])
-        for c in range(3):
+        for c in range(4):
             shrink(1, c)
         second(0, 0, 512, 1)
         first(1, 5, 7)
-        second(0, 512, 512, 0)
-        quantise_x(1)
-        weave(2)
+        second(1, 0, 512, 0)
+        weave(1, 0)
+        weave(1, 1)
+        quantise_x(1, 0)
         empty(0, 0, 512)
         store(0, 0, 512)
-        shrink(1, 3)
+        first(1, 6, 3)
+        second(0, 512, 512, 6)
+        shrink(1, 4)
+        empty(1, 0, 512)
+        store(1, 0, 512)
+        first(1, 7, 2)
+        second(1, 512, 512, 5)
+        quantise_x(1, 1)
+        weave(2, 0)
+        shrink(1, 5)
+        shrink(1, 6, True)
         empty(0, 512, 512)
         store(0, 512, 512)
-        first(1, 6, 3)
-        first(1, 7, 6)
-        quantise_x(2)
-        shrink(1, 4, True)
-        second(1, 0, 512, 2)
-        second(1, 512, 512, 5)
-        shrink(1, 5)
-        weave(3)
-        shrink(1, 6)
         shrink(1, 7, True)
-        for th in range(2):
-            empty(1, 512 * th, 512)
-            store(1, 512 * th, 512)
-        quantise_x(3)
-        rotation = (1, 0, 4, 7, 3, 6, 2, 5)
-        weave(4)
+        quantise_x(2, 0)
+        weave(2, 1)
+        empty(1, 512, 512)
+        store(1, 512, 512)
+        weave(3, 0)
+        quantise_x(2, 1)
+        weave(3, 1)
+        quantise_x(3, 0)
+        quantise_x(3, 1)
+        rotation = (1, 4, 0, 7, 6, 3, 5, 2)
         for r in range(2, 7):
             for th in range(2):
                 second(r, 512 * th, 512, rotation[(2 * r - 4 + th) % 8])
-            if r + 2 < 8:
-                quantise_x(r + 2)
-            if r + 3 < 8:
-                weave(r + 3)
-            for th in range(2):
-                empty(r, 512 * th, 512, r >= 5 and th == 1)
-                store(r, 512 * th, 512)
-        second(7, 0, 512, 4)
+                empty(r, 512 * th, 512, r >= 4 and th == 1)
+                if r == 2:
+                    store(r, 512 * th, 512)
+            if r > 2:
+                store(r, 0, N)
+        second(7, 0, 512, 0)
         second(7, 512, 256, 7)
-        second(7, 768, 256, 3)
+        second(7, 768, 256, 6)
         empty(7, 0, 512)
         store(7, 0, 512)
         empty(7, 512, 256, True)
-        store(7, 512, 256)
         empty(7, 768, 256)
-        store(7, 768, 256)
+        store(7, 512, 512)

@@ -16,9 +16,11 @@ ACT = mybir.ActivationFunctionType
 
 P = 128
 N = 1024
+PASS = 512
+PAIR = 2 * P
+TILES = N // P
 CONC = 0.25
 H = (CONC**2) ** 0.35 * float(N) ** (-0.35)
-WARM = (4, 2, 2)
 FLOPS = 2 * 2 * N * N * N
 
 
@@ -32,63 +34,84 @@ def tile_quadraticinverseshrinkagesignalpnl_w4_kernel(
         psum = ctx.enter_context(tc.psum_pool(name="psum", bufs=1))
         ctx.enter_context(tc.manual_schedule())
 
-        def bank(b, shape):
-            return psum.tile(shape, F32, name="bank", tag="bank%d" % b)
+        free_banks = list(range(8))
+        in_psum = {}
 
-        lam_c = keep.tile([P, 8], BF16, name="lam_c")
-        scale_c = keep.tile([P, 8], F32, name="scale_c")
-        tilt_c = keep.tile([P, 8], BF16, name="tilt_c", tag="uw0", align_bytes=64)
-        q_raw = [keep.tile([P, 2, N], BF16, name="q_raw%d" % d) for d in range(4)]
-        s_raw = [keep.tile([P, 2, N], U8, name="s_raw%d" % d) for d in range(4)]
-        uw_raw = keep.tile([P, 2, 2 * N], U8, name="uw_raw")
-        us_raw = keep.tile([P, 2, N], U8, name="us_raw")
+        def take_bank(key, shape):
+            number = free_banks[0]
+            free_banks.remove(number)
+            in_psum[key] = (psum.tile(shape, F32, name="bank", tag="bank%d" % number), number)
+            return in_psum[key][0]
+
+        def give_bank(key):
+            free_banks.append(in_psum[key][1])
+
+        def copy_on(on_vector):
+            return nc.vector.tensor_copy if on_vector else nc.scalar.copy
 
         ident = keep.tile([P, P], F32, name="ident")
         ones = keep.tile([P, P], F32, name="ones")
         nc.gpsimd.memset(ones[:], 1.0)
         make_identity(nc, ident[:])
 
-        def stoke(count, bk=6):
-            b = bank(bk, [P, P])
+        def warm_up(count):
+            scratch = take_bank("warm", [P, P])
             for n in range(count):
-                nc.tensor.matmul(b[:], lhsT=ones[:], rhs=ones[:], start=True, stop=True)
+                nc.tensor.matmul(scratch[:], lhsT=ones[:], rhs=ones[:], start=True, stop=True)
+            give_bank("warm")
 
-        stoke(WARM[0])
+        warm_up(3)
+
+        lam_c = keep.tile([P, TILES], BF16, name="lam_c")
+        scale_c = keep.tile([P, TILES], F32, name="scale_c")
+        tilt_c = keep.tile([P, TILES], BF16, name="tilt_c", tag="tilt_then_u", align_bytes=64)
+        q_raw = [keep.tile([P, 2, N], BF16, name="q_raw%d" % d) for d in range(4)]
+        s_raw = [keep.tile([P, 2, N], U8, name="s_raw%d" % d) for d in range(4)]
+        uw_raw = keep.tile([P, 2, 2 * N], U8, name="uw_raw")
+        us_raw = keep.tile([P, 2, N], U8, name="us_raw")
+
+        def by_channel_tile(vector):
+            return vector.rearrange("(g p t) -> p g t", g=2, t=4)
 
         def load_q(d):
-            nc.sync.dma_start(out=q_raw[d][:], in_=q[256 * d : 256 * (d + 1), :].rearrange("(a p) k -> p a k", p=P))
+            nc.sync.dma_start(out=q_raw[d][:], in_=q[PAIR * d : PAIR * (d + 1), :].rearrange("(a p) k -> p a k", p=P))
 
         def load_s(d):
-            nc.sync.dma_start(out=s_raw[d][:], in_=signals_bytes[256 * d : 256 * (d + 1), :].rearrange("(p a) k -> p a k", a=2))
+            nc.sync.dma_start(out=s_raw[d][:], in_=signals_bytes[PAIR * d : PAIR * (d + 1), :].rearrange("(p a) k -> p a k", a=2))
 
-        nc.sync.dma_start(out=lam_c[:].rearrange("p (g t) -> p g t", g=2), in_=lam.rearrange("(g p t) -> p g t", g=2, t=4))
-        nc.scalar.dma_start(out=scale_c[:].rearrange("p (g t) -> p g t", g=2), in_=signals_scale.rearrange("o (g p t) -> p (o g) t", g=2, t=4))
+        nc.sync.dma_start(out=lam_c[:].rearrange("p (g t) -> p g t", g=2), in_=by_channel_tile(lam))
+        nc.scalar.dma_start(out=scale_c[:].rearrange("p (g t) -> p g t", g=2), in_=by_channel_tile(signals_scale.rearrange("o k -> (o k)")))
         load_q(0)
         load_s(0)
-        nc.sync.dma_start(out=tilt_c[:].rearrange("p (g t) -> p g t", g=2), in_=tilt.rearrange("(g p t) -> p g t", g=2, t=4))
+        nc.sync.dma_start(out=tilt_c[:].rearrange("p (g t) -> p g t", g=2), in_=by_channel_tile(tilt))
         load_s(1)
         load_q(1)
         load_q(2)
 
-        warm = keep.tile([P, 2], F32, name="warm")
-        nc.vector.memset(warm[:, 0:1], 1.0)
-        nc.scalar.activation(out=warm[:, 1:2], in_=warm[:, 0:1], func=ACT.Abs_reciprocal_sqrt)
+        table_probe = keep.tile([P, 2], F32, name="table_probe")
+        nc.vector.memset(table_probe[:, 0:1], 1.0)
+        nc.scalar.activation(out=table_probe[:, 1:2], in_=table_probe[:, 0:1], func=ACT.Abs_reciprocal_sqrt)
 
-        tab_a = keep.tile([P, 4, 16, 8, 2], BF16, name="tab_a")
-        tab_b = keep.tile([P, 4, 16, 8, 2], BF16, name="tab_b")
+        piece_a = keep.tile([P, 4, 16, 8, 2], BF16, name="piece_a")
+        piece_b = keep.tile([P, 4, 16, 8, 2], BF16, name="piece_b")
+        words_a = piece_a[:].bitcast(F32).rearrange("p c l s o -> p c l (s o)")
+        words_b = piece_b[:].bitcast(F32).rearrange("p c l s o -> p c l (s o)")
+        upper, lower, both_runs = slice(0, 4), slice(4, 8), slice(0, 8)
+
         nc.vector.memset(us_raw[:].bitcast(I32), 0)
-        for tab in (tab_b, tab_a):
-            nc.vector.memset(tab[:].rearrange("p c l s e -> p (c l s e)").bitcast(I32), 0)
-        for tab, levels, slot, value in (
-            (tab_b, slice(0, 8), 0, 1.0),
-            (tab_b, slice(0, 4), 3, 2.0),
-            (tab_b, slice(4, 8), 3, 1.0),
-            (tab_b, slice(4, 8), 5, 1.0),
-            (tab_a, slice(0, 4), 4, 1.0),
-            (tab_a, slice(0, 4), 7, 2.0),
-            (tab_a, slice(4, 8), 7, 1.0),
+        for table in (piece_b, piece_a):
+            nc.vector.memset(table[:].rearrange("p c l s e -> p (c l s e)").bitcast(I32), 0)
+        for table, levels, slot, value in (
+            (piece_b, both_runs, 0, 1.0),
+            (piece_b, upper, 3, 2.0),
+            (piece_b, lower, 3, 1.0),
+            (piece_b, lower, 5, 1.0),
+            (piece_a, upper, 4, 1.0),
+            (piece_a, upper, 7, 2.0),
+            (piece_a, lower, 7, 1.0),
         ):
-            nc.vector.memset(tab[:, :, levels, slot, :], value)
+            nc.vector.memset(table[:, :, levels, slot, :], value)
+
         nc.sync.dma_start(out=uw_raw[:].bitcast(I32), in_=u_words.rearrange("g p n -> p g n").bitcast(I32))
         for quad in range(4):
             nc.sync.dma_start(
@@ -99,407 +122,402 @@ def tile_quadraticinverseshrinkagesignalpnl_w4_kernel(
         load_q(3)
         load_s(3)
 
-        words_a = tab_a[:].bitcast(F32).rearrange("p c l s o -> p c l (s o)")
-        words_b = tab_b[:].bitcast(F32).rearrange("p c l s o -> p c l (s o)")
-
-        base = keep.tile([P, 3, 8], F32, name="base")
-        hl = keep.tile([P, 2, 2, 8], BF16, name="hl")
-        z = keep.tile([P, 10, 8], F32, name="z")
-        rest = keep.tile([P, 10, 8], F32, name="rest")
-        y = keep.tile([P, 3, 10, 8], BF16, name="y")
-        lam32 = keep.tile([P, 8], F32, name="lam32")
-        lam_sum = keep.tile([P, 1], F32, name="lam_sum")
-        inv_lam = keep.tile([P, 8], F32, name="inv_lam")
-        arg_scale = keep.tile([P, 8], F32, name="arg_scale")
-        arg_bias = keep.tile([P, 8], F32, name="arg_bias")
-        h_lam = keep.tile([P, 8], F32, name="h_lam")
-        inv_total = keep.tile([P, 1], F32, name="inv_total")
-        weight = keep.tile([P, 8], F32, name="weight")
-        scale_row = keep.tile([P, N], F32, name="scale_row")
-
         lam_pairs = lam_c[:].rearrange("p (c e) -> p c e", e=2)
-        for tab, levels, slot in ((tab_b, slice(0, 8), 1), (tab_b, slice(4, 8), 4), (tab_a, slice(0, 4), 5)):
-            count = levels.stop - levels.start
+        for table, levels, slot in ((piece_b, both_runs, 1), (piece_b, lower, 4), (piece_a, upper, 5)):
             nc.scalar.activation(
-                out=tab[:, :, levels, slot, :],
-                in_=lam_pairs.unsqueeze(2).to_broadcast([P, 4, count, 2]),
+                out=table[:, :, levels, slot, :],
+                in_=lam_pairs.unsqueeze(2).to_broadcast([P, 4, levels.stop - levels.start, 2]),
                 func=ACT.Copy,
                 scale=-4.0,
             )
 
-        scale_banks = []
+        scale_row = keep.tile([P, N], F32, name="scale_row")
         for g in range(2):
-            sb = bank(g, [P, 4, P])
-            scale_banks.append(sb)
+            spread = take_bank(("scale", g), [P, 4, P])
             for t in range(4):
-                nc.tensor.transpose(sb[:, t, :], scale_c[:, 4 * g + t : 4 * g + t + 1].to_broadcast([P, P]), ident[:])
+                nc.tensor.transpose(spread[:, t, :], scale_c[:, 4 * g + t : 4 * g + t + 1].to_broadcast([P, P]), ident[:])
+
+        base = keep.tile([P, 3, TILES], F32, name="base")
+        halves = keep.tile([P, 2, 2, TILES], BF16, name="halves")
+        whole = keep.tile([P, 10, TILES], F32, name="whole")
+        remainder = keep.tile([P, 10, TILES], F32, name="remainder")
+        pieces = keep.tile([P, 3, 10, TILES], BF16, name="pieces")
+        lam32 = keep.tile([P, TILES], F32, name="lam32")
+        lam_part = keep.tile([P, 1], F32, name="lam_part")
+        inv_lam = keep.tile([P, TILES], F32, name="inv_lam")
+        arg_scale = keep.tile([P, TILES], F32, name="arg_scale")
+        arg_bias = keep.tile([P, TILES], F32, name="arg_bias")
+        h_lam = keep.tile([P, TILES], F32, name="h_lam")
 
         nc.vector.tensor_tensor(out=base[:, 1, :], in0=lam_c[:], in1=lam_c[:], op=ALU.mult)
         nc.vector.scalar_tensor_tensor(out=base[:, 0, :], in0=lam_c[:], scalar=2.0 * H * H, in1=lam_c[:], op0=ALU.mult, op1=ALU.mult)
         nc.vector.tensor_scalar(out=base[:, 2, :], in0=lam_c[:], scalar1=0.5, scalar2=None, op0=ALU.mult)
-        nc.vector.tensor_scalar(out=lam32[:], in0=lam_c[:], scalar1=1.0, scalar2=None, op0=ALU.mult, op1=ALU.add, accum_out=lam_sum[:])
-        nc.vector.tensor_copy(out=hl[:, 0], in_=base[:, 0:2, :])
-        nc.vector.tensor_tensor(out=z[:, 1, :], in0=base[:, 1, :], in1=lam_c[:], op=ALU.mult)
-        nc.vector.tensor_scalar(out=z[:, 2, :], in0=base[:, 1, :], scalar1=6.0, scalar2=None, op0=ALU.mult)
-        nc.vector.tensor_tensor(out=hl[:, 1], in0=base[:, 0:2, :], in1=hl[:, 0], op=ALU.subtract)
+        nc.vector.tensor_scalar(out=lam32[:], in0=lam_c[:], scalar1=1.0, scalar2=None, op0=ALU.mult, op1=ALU.add, accum_out=lam_part[:])
+        nc.vector.tensor_copy(out=halves[:, 0], in_=base[:, 0:2, :])
+        nc.vector.tensor_tensor(out=whole[:, 1, :], in0=base[:, 1, :], in1=lam_c[:], op=ALU.mult)
+        nc.vector.tensor_scalar(out=whole[:, 2, :], in0=base[:, 1, :], scalar1=6.0, scalar2=None, op0=ALU.mult)
+        nc.vector.tensor_tensor(out=halves[:, 1], in0=base[:, 0:2, :], in1=halves[:, 0], op=ALU.subtract)
         nc.vector.reciprocal(out=inv_lam[:], in_=lam32[:])
         nc.vector.tensor_scalar(out=arg_bias[:], in0=base[:, 1, :], scalar1=(H * H * N / CONC) ** 2, scalar2=None, op0=ALU.mult)
-        nc.vector.tensor_tensor(out=z[:, 0:7:6, :], in0=hl[:, 0:1, 1, :].to_broadcast([P, 2, 8]), in1=hl[:, :, 1, :], op=ALU.mult)
-        nc.vector.tensor_tensor(out=z[:, 9, :], in0=hl[:, 1, 1, :], in1=hl[:, 1, 1, :], op=ALU.mult)
+        nc.vector.tensor_tensor(out=whole[:, 0:7:6, :], in0=halves[:, 0:1, 1, :].to_broadcast([P, 2, TILES]), in1=halves[:, :, 1, :], op=ALU.mult)
+        nc.vector.tensor_tensor(out=whole[:, 9, :], in0=halves[:, 1, 1, :], in1=halves[:, 1, 1, :], op=ALU.mult)
         nc.vector.tensor_tensor(
-            out=z[:, 3:9, :].rearrange("p (i j) c -> p i j c", j=2)[:, 0:3:2],
-            in0=hl[:, :, 0:1, :].to_broadcast([P, 2, 2, 8]),
-            in1=base[:, 1:3, :].unsqueeze(1).to_broadcast([P, 2, 2, 8]),
+            out=whole[:, 3:9, :].rearrange("p (i j) c -> p i j c", j=2)[:, 0:3:2],
+            in0=halves[:, :, 0:1, :].to_broadcast([P, 2, 2, TILES]),
+            in1=base[:, 1:3, :].unsqueeze(1).to_broadcast([P, 2, 2, TILES]),
             op=ALU.mult,
         )
-        nc.vector.tensor_tensor(out=z[:, 5, :], in0=hl[:, 0, 0, :], in1=hl[:, 1, 0, :], op=ALU.add)
+        nc.vector.tensor_tensor(out=whole[:, 5, :], in0=halves[:, 0, 0, :], in1=halves[:, 1, 0, :], op=ALU.add)
         nc.vector.tensor_copy(
-            out=words_b[:, :, 0:8, 2:7:4],
-            in_=hl[:, :, 1, :].bitcast(F32).rearrange("p s c -> p c s").unsqueeze(2).to_broadcast([P, 4, 8, 2]),
+            out=words_b[:, :, both_runs, 2:7:4],
+            in_=halves[:, :, 1, :].bitcast(F32).rearrange("p s c -> p c s").unsqueeze(2).to_broadcast([P, 4, 8, 2]),
         )
-        nc.vector.tensor_copy(out=y[:, 0], in_=z[:])
+        nc.vector.tensor_copy(out=pieces[:, 0], in_=whole[:])
         nc.vector.scalar_tensor_tensor(out=arg_scale[:], in0=inv_lam[:], scalar=(N / CONC) ** 2, in1=inv_lam[:], op0=ALU.mult, op1=ALU.mult)
         nc.vector.tensor_scalar(out=h_lam[:], in0=lam_c[:], scalar1=H, scalar2=None, op0=ALU.mult)
-        nc.vector.tensor_tensor(out=y[:, 1], in0=z[:], in1=y[:, 0], op=ALU.subtract)
-        nc.vector.tensor_tensor(out=rest[:], in0=z[:], in1=y[:, 0], op=ALU.subtract)
-
-        nc.vector.tensor_tensor(out=y[:, 2], in0=rest[:], in1=y[:, 1], op=ALU.subtract)
-
-        yw = y[:].bitcast(F32).rearrange("p l q c -> p c l q")
-        nc.vector.tensor_copy(out=words_b[:, :, 0:3, 4:6], in_=yw[:, :, :, 0:2])
-        nc.vector.tensor_copy(
-            out=words_b[:, :, 0:8, 7].rearrange("p c (k l) -> p c k l", k=2)[:, :, :, 1:4],
-            in_=yw[:, :, :, 6:10:3].rearrange("p c l k -> p c k l"),
-        )
-        nc.vector.tensor_copy(
-            out=words_a[:, :, 0:8, 0:3].rearrange("p c (k l) s -> p c k l s", k=2)[:, :, :, 0:3, :],
-            in_=yw[:, :, :, 0:6].rearrange("p c l (k s) -> p c k l s", k=2),
-        )
-        nc.vector.tensor_copy(out=words_a[:, :, 5:8, 3:6], in_=yw[:, :, :, 7:10])
-        nc.vector.tensor_copy(
-            out=words_a[:, :, 0:8, 6].rearrange("p c (k l) -> p c k l", k=2)[:, :, :, 1:4],
-            in_=yw[:, :, :, 2:6:3].rearrange("p c l k -> p c k l"),
-        )
-        nc.vector.tensor_copy(out=words_a[:, :, 1:4, 3], in_=yw[:, :, :, 6])
+        nc.vector.tensor_tensor(out=pieces[:, 1], in0=whole[:], in1=pieces[:, 0], op=ALU.subtract)
+        nc.vector.tensor_tensor(out=remainder[:], in0=whole[:], in1=pieces[:, 0], op=ALU.subtract)
+        nc.vector.tensor_tensor(out=pieces[:, 2], in0=remainder[:], in1=pieces[:, 1], op=ALU.subtract)
 
         for g in range(2):
             nc.scalar.copy(
-                out=scale_row[:, 512 * g : 512 * (g + 1)].rearrange("p (n t) -> p n t", t=4),
-                in_=scale_banks[g][:].rearrange("p t n -> p n t"),
+                out=scale_row[:, PASS * g : PASS * (g + 1)].rearrange("p (n t) -> p n t", t=4),
+                in_=in_psum[("scale", g)][0][:].rearrange("p t n -> p n t"),
             )
+            give_bank(("scale", g))
 
-        q_grp = [keep.tile([P, 2, 256, 2], F32, name="q_grp%d" % d, align_bytes=64) for d in range(4)]
-        s_grp = [keep.tile([P, 2, 256, 2], F32, name="s_grp%d" % d, tag="s_grp%d" % d, align_bytes=64) for d in range(4)]
-        q_codes = [keep.tile([P, 2, 512], U32, name="q_codes%d" % h, align_bytes=64) for h in range(2)]
-        q_scales = [keep.tile([P, 2, 512], U8, name="q_scales%d" % h, align_bytes=64) for h in range(2)]
-        s_codes = [keep.tile([P, 2, w], U32, name="s_codes%d" % h, align_bytes=64) for h, w in enumerate((512, 512))]
-        s_scales = [keep.tile([P, 2, w], U8, name="s_scales%d" % h, align_bytes=64) for h, w in enumerate((512, 512))]
-        s_wide = [keep.tile([P, N], BF16, name="s_wide%d" % r) for r in range(8)]
-        held = {}
+        piece_words = pieces[:].bitcast(F32).rearrange("p l q c -> p c l q")
+        nc.vector.tensor_copy(out=words_b[:, :, 0:3, 4:6], in_=piece_words[:, :, :, 0:2])
+        nc.vector.tensor_copy(
+            out=words_b[:, :, both_runs, 7].rearrange("p c (k l) -> p c k l", k=2)[:, :, :, 1:4],
+            in_=piece_words[:, :, :, 6:10:3].rearrange("p c l k -> p c k l"),
+        )
+        nc.scalar.copy(
+            out=words_a[:, :, both_runs, 0:3].rearrange("p c (k l) s -> p c k l s", k=2)[:, :, :, 0:3, :],
+            in_=piece_words[:, :, :, 0:6].rearrange("p c l (k s) -> p c k l s", k=2),
+        )
+        nc.scalar.copy(out=words_a[:, :, 5:8, 3:6], in_=piece_words[:, :, :, 7:10])
+        nc.scalar.copy(
+            out=words_a[:, :, both_runs, 6].rearrange("p c (k l) -> p c k l", k=2)[:, :, :, 1:4],
+            in_=piece_words[:, :, :, 2:6:3].rearrange("p c l k -> p c k l"),
+        )
+        nc.scalar.copy(out=words_a[:, :, 1:4, 3], in_=piece_words[:, :, :, 6])
+
+        s_wide = [keep.tile([P, N], BF16, name="s_wide%d" % r) for r in range(TILES)]
+        grouped, codes, scales = {}, {}, {}
+        for kind in ("q", "s"):
+            grouped[kind] = [keep.tile([P, 2, PAIR, 2], F32, name="%s_grouped%d" % (kind, d), tag="%s_grouped%d" % (kind, d), align_bytes=64) for d in range(4)]
+            codes[kind] = [keep.tile([P, 2, PASS], U32, name="%s_codes%d" % (kind, half), align_bytes=64) for half in range(2)]
+            scales[kind] = [keep.tile([P, 2, PASS], U8, name="%s_scales%d" % (kind, half), align_bytes=64) for half in range(2)]
 
         def widen(r, lo=0, hi=N):
             nc.vector.tensor_tensor(out=s_wide[r][:, lo:hi], in0=s_raw[r // 2][:, r % 2, lo:hi].bitcast(FP8), in1=scale_row[:, lo:hi], op=ALU.mult)
 
-        def flip(kind, r, bk):
+        def turn_words(dst, rows, g, u):
+            nc.tensor.transpose(dst, rows.bitcast(F32)[:, 256 * g + u : 256 * (g + 1) : 2], ident[:])
+
+        def turn(kind, r):
             rows = q_raw[r // 2][:, r % 2, :] if kind == "q" else s_wide[r][:]
-            words = rows.bitcast(F32)
-            b = bank(bk, [P, 2, 2, P])
-            held[(kind, r)] = b
+            turned = take_bank((kind, r), [P, 2, 2, P])
             for g in range(2):
                 for u in range(2):
-                    nc.tensor.transpose(b[:, g, u, :], words[:, 256 * g + u : 256 * (g + 1) : 2], ident[:])
+                    turn_words(turned[:, g, u, :], rows, g, u)
 
         def group(kind, r, on_vector=False):
-            grp = (q_grp if kind == "q" else s_grp)[r // 2]
-            (nc.vector.tensor_copy if on_vector else nc.scalar.copy)(out=grp[:, :, P * (r % 2) : P * (r % 2 + 1), :], in_=held[(kind, r)][:].rearrange("p g u r -> p g r u"))
+            copy_on(on_vector)(
+                out=grouped[kind][r // 2][:, :, P * (r % 2) : P * (r % 2 + 1), :],
+                in_=in_psum[(kind, r)][0][:].rearrange("p g u r -> p g r u"),
+            )
+            give_bank((kind, r))
 
         def quantise(kind, d, g):
-            grp, codes, scales = (q_grp, q_codes, q_scales) if kind == "q" else (s_grp, s_codes, s_scales)
-            h, lo = d // 2, 256 * (d % 2)
-            cols = slice(lo, lo + 256)
+            cols = slice(PAIR * (d % 2), PAIR * (d % 2 + 1))
             nc.vector.quantize_mx(
-                out=codes[h][:, g, cols].bitcast(FP8X4),
-                scales=scales[h][:, g, cols],
-                in_=grp[d][:, g].rearrange("p r u -> p (r u)").bitcast(BF16),
+                out=codes[kind][d // 2][:, g, cols].bitcast(FP8X4),
+                scales=scales[kind][d // 2][:, g, cols],
+                in_=grouped[kind][d][:, g].rearrange("p r u -> p (r u)").bitcast(BF16),
             )
 
-        lam_bank = bank(7, [P, 4, P])
-        lam_words = lam_c[:].bitcast(F32)
-        lam_row = lam_bank[:].rearrange("p c n -> p (c n)").bitcast(BF16)
-        stoke(WARM[1])
-        flip("q", 0, 2)
-        stoke(WARM[2])
+        warm_up(2)
+        turn("q", 0)
+        warm_up(2)
         group("q", 0)
+        for r in range(3):
+            widen(r)
 
         rows_a = keep.tile([P, 4, P], F32, name="rows_a")
         rows_b = keep.tile([P, 4, P], F32, name="rows_b")
-
-        def table(words, rows, lo, hi, bk, on_vector):
-            b = bank(bk, [P, hi - lo, P])
+        for words, rows, lo, hi in ((words_b, rows_b, 0, 2), (words_a, rows_a, 0, 1), (words_b, rows_b, 2, 4), (words_a, rows_a, 1, 4)):
+            turned_table = take_bank("table", [P, hi - lo, P])
             for cp in range(lo, hi):
-                nc.tensor.transpose(b[:, cp - lo, :], words[:, cp].rearrange("p l s -> p (l s)"), ident[:])
-            if on_vector:
-                nc.vector.tensor_copy(out=rows[:, lo:hi], in_=b[:])
-            else:
-                nc.scalar.copy(out=rows[:, lo:hi], in_=b[:])
+                nc.tensor.transpose(turned_table[:, cp - lo, :], words[:, cp].rearrange("p l s -> p (l s)"), ident[:])
+            nc.scalar.copy(out=rows[:, lo:hi], in_=turned_table[:])
+            give_bank("table")
+        pair_moving = rows_b[:].rearrange("p c n -> p (c n)").bitcast(BF16)
+        pair_stationary = rows_a[:].bitcast(BF16)
 
-        widen(0)
-        widen(1)
-        widen(2)
-        table(words_b, rows_b, 0, 2, 0, False)
-        table(words_a, rows_a, 0, 1, 4, False)
-        table(words_b, rows_b, 2, 4, 5, False)
-        table(words_a, rows_a, 1, 4, 6, False)
+        lam_spread = take_bank("lam", [P, 4, P])
         for cp in range(4):
-            nc.tensor.transpose(lam_bank[:, cp, :], lam_words[:, cp : cp + 1].to_broadcast([P, P]), ident[:])
-        total_bank = bank(3, [P, 1])
-        nc.tensor.matmul(total_bank[:], lhsT=ones[:], rhs=lam_sum[:], start=True, stop=True)
-        nc.vector.reciprocal(out=inv_total[:], in_=total_bank[:])
+            nc.tensor.transpose(lam_spread[:, cp, :], lam_c[:].bitcast(F32)[:, cp : cp + 1].to_broadcast([P, P]), ident[:])
+        lam_row = lam_spread[:].rearrange("p c n -> p (c n)").bitcast(BF16)
+
+        def sum_over_partitions(key, column):
+            total = take_bank(key, [P, 1])
+            nc.tensor.matmul(total[:], lhsT=ones[:], rhs=column, start=True, stop=True)
+            return total
+
+        inv_lam_sum = keep.tile([P, 1], F32, name="inv_lam_sum")
+        weight = keep.tile([P, TILES], F32, name="weight")
+        nc.vector.reciprocal(out=inv_lam_sum[:], in_=sum_over_partitions("lam_sum", lam_part[:])[:])
+        give_bank("lam_sum")
         widen(3)
-        nc.vector.scalar_tensor_tensor(out=weight[:], in0=tilt_c[:], scalar=inv_total[:], in1=inv_lam[:], op0=ALU.mult, op1=ALU.mult)
+        nc.vector.scalar_tensor_tensor(out=weight[:], in0=tilt_c[:], scalar=inv_lam_sum[:], in1=inv_lam[:], op0=ALU.mult, op1=ALU.mult)
 
-        moving = rows_b[:].rearrange("p c n -> p (c n)").bitcast(BF16)
-        stationary = rows_a[:].bitcast(BF16)
-        sums = keep.tile([P, 8, 2], F32, name="sums")
-        tilted = keep.tile([P, 8], F32, name="tilted")
+        u_codes, u_planes = {}, {}
 
-        def pairs(c, half):
-            if half == 0:
-                held[("rec", c)] = ring.tile([P, N], F32, name="rec", bufs=4)
-            rec = held[("rec", c)]
-            b = bank((0, 1, 6)[(2 * c + half) % 3], [P, 512])
-            cols = slice(512 * half, 512 * (half + 1))
-            nc.tensor.matmul(b[:], lhsT=stationary[:, c // 2, c % 2 :: 2], rhs=moving[:, cols], start=True, stop=True)
-            nc.scalar.activation(
-                out=rec[:, cols], in_=b[:], func=ACT.Abs_reciprocal_sqrt,
-                scale=arg_scale[:, c : c + 1], bias=arg_bias[:, c : c + 1], accum_out=sums[:, c, half : half + 1],
-            )
-
-        def skew(c):
-            rec = held[("rec", c)]
-            nc.vector.scalar_tensor_tensor(
-                out=rec[:], in0=lam_row, scalar=lam32[:, c : c + 1], in1=rec[:],
-                op0=ALU.subtract, op1=ALU.mult, accum_out=tilted[:, c : c + 1],
-            )
-
-
-        def reorder_u(gx, tag):
-            uw = keep.tile([P, 2, N], U8, name="uw%d" % gx, tag=tag, align_bytes=64)
-            held[("uw", gx)] = uw
+        def order_u_words(gx, slot):
+            u_codes[gx] = keep.tile([P, 2, N], U8, name="u_codes%d" % gx, tag=slot, align_bytes=64)
             nc.gpsimd.tensor_copy(
-                out=uw[:].rearrange("p g (t m b) -> p g t m b", t=4, b=2),
+                out=u_codes[gx][:].rearrange("p g (t m b) -> p g t m b", t=4, b=2),
                 in_=uw_raw[:, :, N * gx : N * (gx + 1)].rearrange("p g (m t b) -> p g t m b", t=4, b=2),
             )
 
-        def reorder_scales(gx, tag):
-            held[("us", gx)] = keep.tile([P, 2, 512], U8, name="us%d" % gx, tag=tag, align_bytes=64)
+        def order_u_scales(gx, slot):
+            u_planes[gx] = keep.tile([P, 2, PASS], U8, name="u_planes%d" % gx, tag=slot, align_bytes=64)
             nc.gpsimd.tensor_copy(
-                out=held[("us", gx)][:].rearrange("p g (t m) -> p g t m", t=4),
-                in_=us_raw[:, :, 512 * gx : 512 * (gx + 1)].rearrange("p g (m t) -> p g t m", t=4),
+                out=u_planes[gx][:].rearrange("p g (t m) -> p g t m", t=4),
+                in_=us_raw[:, :, PASS * gx : PASS * (gx + 1)].rearrange("p g (m t) -> p g t m", t=4),
             )
 
-        x_planes = [keep.tile([P, 2, 4, 512], BF16, name="x_planes%d" % h) for h in range(2)]
-        factor = keep.tile([P, 8], F32, name="factor")
+        order_u_words(0, "tilt_then_u")
+        order_u_scales(0, "u_planes0")
+        order_u_words(1, "u_codes1")
 
-        def first(h, c, bk, passes=(0, 1)):
+        row_sums = keep.tile([P, TILES, 2], F32, name="row_sums")
+        skew_sums = keep.tile([P, TILES], F32, name="skew_sums")
+        inv_den = {}
+
+        def invert_pairs(c):
+            inv_den[c] = ring.tile([P, N], F32, name="inv_den", bufs=4)
+            for part in range(2):
+                cols = slice(PASS * part, PASS * (part + 1))
+                square = take_bank("pairs", [P, PASS])
+                nc.tensor.matmul(square[:], lhsT=pair_stationary[:, c // 2, c % 2 :: 2], rhs=pair_moving[:, cols], start=True, stop=True)
+                nc.scalar.activation(
+                    out=inv_den[c][:, cols],
+                    in_=square[:],
+                    func=ACT.Abs_reciprocal_sqrt,
+                    scale=arg_scale[:, c : c + 1],
+                    bias=arg_bias[:, c : c + 1],
+                    accum_out=row_sums[:, c, part : part + 1],
+                )
+                give_bank("pairs")
+
+        def skew(c):
+            nc.vector.scalar_tensor_tensor(
+                out=inv_den[c][:],
+                in0=lam_row,
+                scalar=lam32[:, c : c + 1],
+                in1=inv_den[c][:],
+                op0=ALU.subtract,
+                op1=ALU.mult,
+                accum_out=skew_sums[:, c : c + 1],
+            )
+
+        for c in range(TILES):
+            invert_pairs(c)
+            if 2 <= c < 6:
+                group("s", c - 2, on_vector=(c == 2))
+            turn(*(("s", c) if c < 4 else ("q", c - 3)))
+            if c >= 1:
+                skew(c - 1)
+            if c == TILES - 2:
+                for g in range(2):
+                    for d in range(2):
+                        quantise("s", d, g)
+                order_u_scales(1, "s_grouped1")
+        skew(TILES - 1)
+
+        factor = keep.tile([P, TILES], F32, name="factor")
+        x_planes = [[keep.tile([P, 4, PASS], BF16, name="x_planes%d%d" % (half, gx)) for gx in range(2)] for half in range(2)]
+        x_codes = [keep.tile([P, 2, PAIR], U32, name="x_codes%d" % d, align_bytes=64) for d in range(4)]
+        x_scales = [keep.tile([P, 2, PAIR], U8, name="x_scales%d" % d, align_bytes=64) for d in range(4)]
+        x_grouped, result = {}, {}
+        out_rows = out.rearrange("(d p a) t -> d a p t", p=P, a=2)
+
+        def first(half, c, passes=(0, 1)):
             if 0 in passes:
-                held[("y", h, c)] = bank(bk, [P, 512])
-            b = held[("y", h, c)]
+                take_bank(("y", half, c), [P, PASS])
             for g in passes:
                 nc.tensor.matmul_mx(
-                    b[:],
-                    lhsT=held[("uw", c // 4)][:, g, 256 * (c % 4) : 256 * (c % 4 + 1)].bitcast(FP4X4),
-                    lhsT_scale=held[("us", c // 4)][:, g, P * (c % 4) : P * (c % 4 + 1)],
-                    rhs=s_codes[h][:, g, :].bitcast(FP8X4), rhs_scale=s_scales[h][:, g, :], start=(g == 0), stop=(g == 1),
+                    in_psum[("y", half, c)][0][:],
+                    lhsT=u_codes[c // 4][:, g, 2 * P * (c % 4) : 2 * P * (c % 4 + 1)].bitcast(FP4X4),
+                    lhsT_scale=u_planes[c // 4][:, g, P * (c % 4) : P * (c % 4 + 1)],
+                    rhs=codes["s"][half][:, g, :].bitcast(FP8X4),
+                    rhs_scale=scales["s"][half][:, g, :],
+                    start=(g == 0),
+                    stop=(g == 1),
                 )
 
-        def shrink(h, c, on_vector=False):
+        def shrink(half, c, on_vector=False):
+            plane, y, column = x_planes[half][c // 4][:, c % 4, :], in_psum[("y", half, c)][0][:], factor[:, c : c + 1]
             if on_vector:
-                nc.vector.tensor_scalar(out=x_planes[h][:, c // 4, c % 4, :], in0=held[("y", h, c)][:], scalar1=factor[:, c : c + 1], scalar2=None, op0=ALU.mult)
+                nc.vector.tensor_scalar(out=plane, in0=y, scalar1=column, scalar2=None, op0=ALU.mult)
             else:
-                nc.scalar.activation(out=x_planes[h][:, c // 4, c % 4, :], in_=held[("y", h, c)][:], func=ACT.Copy, scale=factor[:, c : c + 1])
-
-        x_codes = [keep.tile([P, 2, 256], U32, name="x_codes%d" % d, align_bytes=64) for d in range(4)]
-        x_scales = [keep.tile([P, 2, 256], U8, name="x_scales%d" % d, align_bytes=64) for d in range(4)]
+                nc.scalar.activation(out=plane, in_=y, func=ACT.Copy, scale=column)
+            give_bank(("y", half, c))
 
         def weave(d, gx):
-            xg = ring.tile([P, 256, 4], BF16, name="xg", align_bytes=64)
-            held[("xg", d, gx)] = xg
-            nc.vector.tensor_copy(out=xg[:], in_=x_planes[d // 2][:, gx, :, 256 * (d % 2) : 256 * (d % 2 + 1)].rearrange("p t n -> p n t"))
+            x_grouped[(d, gx)] = ring.tile([P, PAIR, 4], BF16, name="x_grouped", align_bytes=64)
+            planes = x_planes[d // 2][gx][:, :, PAIR * (d % 2) : PAIR * (d % 2 + 1)]
+            nc.vector.tensor_copy(out=x_grouped[(d, gx)][:], in_=planes.rearrange("p t n -> p n t"))
 
         def quantise_x(d, gx):
             nc.vector.quantize_mx(
                 out=x_codes[d][:, gx, :].bitcast(FP8X4),
                 scales=x_scales[d][:, gx, :],
-                in_=held[("xg", d, gx)][:].rearrange("p n t -> p (n t)"),
+                in_=x_grouped[(d, gx)][:].rearrange("p n t -> p (n t)"),
             )
 
-        out_rows = out.rearrange("(d p a) t -> d a p t", p=P, a=2)
-
-        def second(r, lo, width, bk):
+        def second(r, lo, width):
             tokens = slice(P * (r % 2), P * (r % 2 + 1))
-            b = bank(bk, [P, width])
-            held[("o", r, lo)] = b
-            cols = slice(lo % 512, lo % 512 + width)
-            for g in range(2):
+            cols = slice(lo % PASS, lo % PASS + width)
+            acc = take_bank(("out", r, lo), [P, width])
+            for gx in range(2):
                 nc.tensor.matmul_mx(
-                    b[:], lhsT=x_codes[r // 2][:, g, tokens].bitcast(FP8X4), lhsT_scale=x_scales[r // 2][:, g, tokens],
-                    rhs=q_codes[lo // 512][:, g, cols].bitcast(FP8X4), rhs_scale=q_scales[lo // 512][:, g, cols], start=(g == 0), stop=(g == 1),
+                    acc[:],
+                    lhsT=x_codes[r // 2][:, gx, tokens].bitcast(FP8X4),
+                    lhsT_scale=x_scales[r // 2][:, gx, tokens],
+                    rhs=codes["q"][lo // PASS][:, gx, cols].bitcast(FP8X4),
+                    rhs_scale=scales["q"][lo // PASS][:, gx, cols],
+                    start=(gx == 0),
+                    stop=(gx == 1),
                 )
 
         def empty(r, lo, width, on_vector=False):
             if lo == 0:
-                held[("out", r)] = ring.tile([P, N], F32, name="o", bufs=4)
-            (nc.vector.tensor_copy if on_vector else nc.scalar.copy)(out=held[("out", r)][:, lo : lo + width], in_=held[("o", r, lo)][:])
+                result[r] = ring.tile([P, N], F32, name="result", bufs=6)
+            copy_on(on_vector)(out=result[r][:, lo : lo + width], in_=in_psum[("out", r, lo)][0][:])
+            give_bank(("out", r, lo))
 
         def store(r, lo, width):
-            nc.sync.dma_start(out=out_rows[r // 2, r % 2, :, lo : lo + width], in_=held[("out", r)][:, lo : lo + width])
+            nc.sync.dma_start(out=out_rows[r // 2, r % 2, :, lo : lo + width], in_=result[r][:, lo : lo + width])
 
-        both = keep.tile([P, 8], F32, name="both")
-        legs = keep.tile([P, 2, 8], F32, name="legs")
-        squares = keep.tile([P, 2, 8], F32, name="squares")
-        denom = keep.tile([P, 8], F32, name="denom")
-        inv_denom = keep.tile([P, 8], F32, name="inv_denom")
-        r_vals = keep.tile([P, 8], F32, name="r_vals")
-        r_sum = keep.tile([P, 1], F32, name="r_sum")
-        unscaled = keep.tile([P, 8], F32, name="unscaled")
-
-        reorder_u(0, "uw0")
-        reorder_scales(0, "us0")
-        reorder_u(1, "uw1")
-        for c in range(8):
-            pairs(c, 0)
-            pairs(c, 1)
-            if 2 <= c < 6:
-                group("s", c - 2, c == 2)
-            flip(*(("s", c) if c < 4 else ("q", c - 3)), 2 + c % 4)
-            if c >= 1:
-                skew(c - 1)
-            if c == 6:
-                for g in range(2):
-                    for d in range(2):
-                        quantise("s", d, g)
-                reorder_scales(1, "s_grp1")
-        skew(7)
         for g in range(2):
             for c in range(3):
-                first(0, c, (1, 6, 0)[c], (g,))
+                first(0, c, (g,))
         group("q", 1)
-        flip("q", 5, 2)
         group("q", 2)
-        first(0, 3, 3)
+        turn("q", 5)
+        turn("q", 6)
         group("q", 3)
-        flip("q", 6, 4)
         group("q", 4)
+        first(0, 3)
+        turn("q", 7)
         group("q", 5)
+        first(0, 4)
         group("q", 6)
-        nc.vector.tensor_tensor(out=both[:], in0=sums[:, :, 0], in1=sums[:, :, 1], op=ALU.add)
-        nc.vector.tensor_scalar(out=legs[:, 0, :], in0=tilted[:], scalar1=CONC - 1.0, scalar2=None, op0=ALU.add)
-        widen(4, 0, 256)
-        nc.vector.tensor_tensor(out=legs[:, 1, :], in0=both[:], in1=h_lam[:], op=ALU.mult)
-        widen(4, 256, 512)
+        give_bank("lam")
+        group("q", 7)
+
+        row_sum = keep.tile([P, TILES], F32, name="row_sum")
+        legs = keep.tile([P, 2, TILES], F32, name="legs")
+        squares = keep.tile([P, 2, TILES], F32, name="squares")
+        g_vals = keep.tile([P, TILES], F32, name="g_vals")
+        inv_g = keep.tile([P, TILES], F32, name="inv_g")
+        r_vals = keep.tile([P, TILES], F32, name="r_vals")
+        r_part = keep.tile([P, 1], F32, name="r_part")
+        unscaled = keep.tile([P, TILES], F32, name="unscaled")
+        quarter = N // 4
+        nc.vector.tensor_tensor(out=row_sum[:], in0=row_sums[:, :, 0], in1=row_sums[:, :, 1], op=ALU.add)
+        nc.vector.tensor_scalar(out=legs[:, 0, :], in0=skew_sums[:], scalar1=CONC - 1.0, scalar2=None, op0=ALU.add)
+        widen(4, 0, quarter)
+        nc.vector.tensor_tensor(out=legs[:, 1, :], in0=row_sum[:], in1=h_lam[:], op=ALU.mult)
+        widen(4, quarter, 2 * quarter)
         nc.vector.tensor_tensor(out=squares[:], in0=legs[:], in1=legs[:], op=ALU.mult)
-        widen(4, 512, 768)
-        nc.vector.tensor_tensor(out=denom[:], in0=squares[:, 0, :], in1=squares[:, 1, :], op=ALU.add)
-        widen(4, 768, N)
-        nc.vector.reciprocal(out=inv_denom[:], in_=denom[:])
-        widen(5, 0, 256)
-        nc.vector.scalar_tensor_tensor(out=r_vals[:], in0=inv_denom[:], scalar=1.0, in1=lam32[:], op0=ALU.mult, op1=ALU.mult, accum_out=r_sum[:])
-        nc.vector.tensor_tensor(out=unscaled[:], in0=denom[:], in1=weight[:], op=ALU.mult)
-        first(0, 4, 5)
-        r_bank = bank(7, [P, 1])
-        nc.tensor.matmul(r_bank[:], lhsT=ones[:], rhs=r_sum[:], start=True, stop=True)
-        widen(5, 256, N)
-        nc.vector.tensor_scalar(out=factor[:], in0=unscaled[:], scalar1=r_bank[:], scalar2=None, op0=ALU.mult)
+        widen(4, 2 * quarter, 3 * quarter)
+        nc.vector.tensor_tensor(out=g_vals[:], in0=squares[:, 0, :], in1=squares[:, 1, :], op=ALU.add)
+        widen(4, 3 * quarter, N)
+        nc.vector.reciprocal(out=inv_g[:], in_=g_vals[:])
+        widen(5, 0, quarter)
+        nc.vector.scalar_tensor_tensor(out=r_vals[:], in0=inv_g[:], scalar=1.0, in1=lam32[:], op0=ALU.mult, op1=ALU.mult, accum_out=r_part[:])
+        nc.vector.tensor_tensor(out=unscaled[:], in0=g_vals[:], in1=weight[:], op=ALU.mult)
+        r_total = sum_over_partitions("r_sum", r_part[:])
+        widen(5, quarter, N)
+        nc.vector.tensor_scalar(out=factor[:], in0=unscaled[:], scalar1=r_total[:], scalar2=None, op0=ALU.mult)
+        give_bank("r_sum")
         widen(6)
         widen(7)
-        first(0, 5, 4)
-        flip("s", 4, 2)
-        flip("s", 5, 7)
+
+        first(0, 5)
+        turn("s", 4)
+        turn("s", 5)
         shrink(0, 0)
         shrink(0, 1)
+        first(0, 6)
         group("s", 4)
         group("s", 5)
-        first(0, 6, 1)
-        flip("s", 6, 6)
-        flip("s", 7, 2)
-        shrink(0, 2)
-        group("s", 6)
-        group("s", 7)
-        first(0, 7, 7)
-        flip("q", 7, 0)
-        quantise("q", 0, 0)
-        quantise("q", 0, 1)
-        quantise("s", 2, 0)
-        quantise("s", 2, 1)
-        shrink(0, 3, True)
-        shrink(0, 4, True)
-        quantise("s", 3, 0)
-        quantise("s", 3, 1)
-        for c in range(5, 8):
-            shrink(0, c)
-        group("q", 7)
-        weave(0, 0)
-        quantise("q", 1, 0)
-        weave(0, 1)
-        quantise_x(0, 0)
-        quantise("q", 1, 1)
-        quantise_x(0, 1)
-        for d in range(2, 4):
+        last_pair = [take_bank(("pass", g), [P, 2, 2, P]) for g in range(2)]
+        for a in range(2):
             for g in range(2):
-                quantise("q", d, g)
+                for u in range(2):
+                    turn_words(last_pair[g][:, u, a, :], s_wide[6 + a][:], g, u)
+        shrink(0, 2)
+        first(0, 7)
+        for kind, d in (("q", 0), ("s", 2)):
+            for g in range(2):
+                quantise(kind, d, g)
+        for g in range(2):
+            copy_on(g == 1)(out=grouped["s"][3][:, g], in_=last_pair[g][:].rearrange("p u a r -> p (a r) u"))
+            give_bank(("pass", g))
+        for g in range(2):
+            quantise("s", 3, g)
+        for c in (3, 4, 5, 7):
+            shrink(0, c)
+        quantise("q", 1, 0)
+        quantise("q", 1, 1)
+        weave(0, 0)
+        quantise("q", 2, 0)
+        quantise("q", 2, 1)
+        shrink(0, 6, on_vector=True)
+        weave(0, 1)
+        for g in range(2):
+            quantise_x(0, g)
+            quantise("q", 3, g)
+        for step in (weave, quantise_x):
+            for gx in range(2):
+                step(1, gx)
+
         for g in range(2):
             for c in range(2):
-                first(1, c, (3, 6)[c], (g,))
-        for c in range(2, 5):
-            first(1, c, (2, 5, 4)[c - 2])
-        for c in range(4):
+                first(1, c, (g,))
+        for c in range(2, TILES):
+            first(1, c)
+        for c in range(TILES - 1):
             shrink(1, c)
-        second(0, 0, 512, 1)
-        first(1, 5, 7)
-        second(1, 0, 512, 0)
-        weave(1, 0)
-        weave(1, 1)
-        quantise_x(1, 0)
-        empty(0, 0, 512)
-        store(0, 0, 512)
-        first(1, 6, 3)
-        second(0, 512, 512, 6)
-        shrink(1, 4)
-        empty(1, 0, 512)
-        store(1, 0, 512)
-        first(1, 7, 2)
-        second(1, 512, 512, 5)
-        quantise_x(1, 1)
         weave(2, 0)
-        shrink(1, 5)
-        shrink(1, 6, True)
-        empty(0, 512, 512)
-        store(0, 512, 512)
-        shrink(1, 7, True)
-        quantise_x(2, 0)
+        second(0, 0, PASS)
+        empty(0, 0, PASS)
+        store(0, 0, PASS)
+        shrink(1, TILES - 1, on_vector=True)
         weave(2, 1)
-        empty(1, 512, 512)
-        store(1, 512, 512)
-        weave(3, 0)
-        quantise_x(2, 1)
-        weave(3, 1)
-        quantise_x(3, 0)
-        quantise_x(3, 1)
-        rotation = (1, 4, 0, 7, 6, 3, 5, 2)
-        for r in range(2, 7):
-            for th in range(2):
-                second(r, 512 * th, 512, rotation[(2 * r - 4 + th) % 8])
-                empty(r, 512 * th, 512, r >= 4 and th == 1)
-                if r == 2:
-                    store(r, 512 * th, 512)
-            if r > 2:
-                store(r, 0, N)
-        second(7, 0, 512, 0)
-        second(7, 512, 256, 7)
-        second(7, 768, 256, 6)
-        empty(7, 0, 512)
-        store(7, 0, 512)
-        empty(7, 512, 256, True)
-        empty(7, 768, 256)
-        store(7, 512, 512)
+        for step, d in ((quantise_x, 2), (weave, 3), (quantise_x, 3)):
+            for gx in range(2):
+                step(d, gx)
+        second(0, PASS, PASS)
+        empty(0, PASS, PASS)
+        store(0, PASS, PASS)
+        for r in range(1, TILES - 1):
+            for lo in (0, PASS):
+                second(r, lo, PASS)
+                empty(r, lo, PASS, on_vector=(r >= 4 and lo == PASS))
+            store(r, 0, N)
+        last = TILES - 1
+        second(last, 0, PASS)
+        second(last, PASS, PASS // 2)
+        second(last, PASS + PASS // 2, PASS // 2)
+        empty(last, 0, PASS)
+        store(last, 0, PASS)
+        empty(last, PASS, PASS // 2, on_vector=True)
+        empty(last, PASS + PASS // 2, PASS // 2)
+        store(last, PASS, PASS)

@@ -54,14 +54,6 @@ def tile_quadraticinverseshrinkagesignalpnl_w4_kernel(
         nc.gpsimd.memset(ones[:], 1.0)
         make_identity(nc, ident[:])
 
-        def warm_up(count):
-            scratch = take_bank("warm", [P, P])
-            for n in range(count):
-                nc.tensor.matmul(scratch[:], lhsT=ones[:], rhs=ones[:], start=True, stop=True)
-            give_bank("warm")
-
-        warm_up(3)
-
         lam_c = keep.tile([P, TILES], BF16, name="lam_c")
         scale_c = keep.tile([P, TILES], F32, name="scale_c")
         tilt_c = keep.tile([P, TILES], BF16, name="tilt_c", tag="tilt_then_u", align_bytes=64)
@@ -238,9 +230,7 @@ def tile_quadraticinverseshrinkagesignalpnl_w4_kernel(
                 in_=grouped[kind][d][:, g].rearrange("p r u -> p (r u)").bitcast(BF16),
             )
 
-        warm_up(2)
         turn("q", 0)
-        warm_up(2)
         group("q", 0)
         for r in range(3):
             widen(r)

from contextlib import ExitStack

import concourse.mybir as mybir
from concourse.masks import make_identity

F32 = mybir.dt.float32
BF16 = mybir.dt.bfloat16
I32 = mybir.dt.int32
U32 = mybir.dt.uint32
U8 = mybir.dt.uint8
FP8 = mybir.dt.float8_e4m3fn
FP8X4 = mybir.dt.float8_e4m3fn_x4
FP4X4 = mybir.dt.float4_e2m1fn_x4
ALU = mybir.AluOpType
ACT = mybir.ActivationFunctionType

P = 128
N = 1024
PASS = 512
PAIR = 2 * P
TILES = N // P
CONC = 0.25
H = (CONC**2) ** 0.35 * float(N) ** (-0.35)
FLOPS = 2 * 2 * N * N * N


def tile_quadraticinverseshrinkagesignalpnl_w4_kernel(
    tc, signals_bytes, signals_scale, u_words, u_scales, lam, tilt, q, out
):
    nc = tc.nc
    with ExitStack() as ctx:
        keep = ctx.enter_context(tc.tile_pool(name="keep", bufs=1))
        ring = ctx.enter_context(tc.tile_pool(name="ring", bufs=3))
        psum = ctx.enter_context(tc.psum_pool(name="psum", bufs=1))
        ctx.enter_context(tc.manual_schedule())

        free_banks = list(range(8))
        in_psum = {}

        def take_bank(key, shape):
            number = free_banks[0]
            free_banks.remove(number)
            in_psum[key] = (psum.tile(shape, F32, name="bank", tag="bank%d" % number), number)
            return in_psum[key][0]

        def give_bank(key):
            free_banks.append(in_psum[key][1])

        def copy_on(on_vector):
            return nc.vector.tensor_copy if on_vector else nc.scalar.copy

        ident = keep.tile([P, P], F32, name="ident")
        ones = keep.tile([P, P], F32, name="ones")
        nc.gpsimd.memset(ones[:], 1.0)
        make_identity(nc, ident[:])

        lam_c = keep.tile([P, TILES], BF16, name="lam_c")
        scale_c = keep.tile([P, TILES], F32, name="scale_c")
        tilt_c = keep.tile([P, TILES], BF16, name="tilt_c", tag="tilt_then_u", align_bytes=64)
        q_raw = [keep.tile([P, 2, N], BF16, name="q_raw%d" % d) for d in range(4)]
        s_raw = [keep.tile([P, 2, N], U8, name="s_raw%d" % d) for d in range(4)]
        uw_raw = keep.tile([P, 2, 2 * N], U8, name="uw_raw")
        us_raw = keep.tile([P, 2, N], U8, name="us_raw")

        def by_channel_tile(vector):
            return vector.rearrange("(g p t) -> p g t", g=2, t=4)

        def load_q(d):
            nc.sync.dma_start(out=q_raw[d][:], in_=q[PAIR * d : PAIR * (d + 1), :].rearrange("(a p) k -> p a k", p=P))

        def load_s(d):
            nc.sync.dma_start(out=s_raw[d][:], in_=signals_bytes[PAIR * d : PAIR * (d + 1), :].rearrange("(p a) k -> p a k", a=2))

        nc.sync.dma_start(out=lam_c[:].rearrange("p (g t) -> p g t", g=2), in_=by_channel_tile(lam))
        nc.scalar.dma_start(out=scale_c[:].rearrange("p (g t) -> p g t", g=2), in_=by_channel_tile(signals_scale.rearrange("o k -> (o k)")))
        load_q(0)
        load_s(0)
        nc.sync.dma_start(out=tilt_c[:].rearrange("p (g t) -> p g t", g=2), in_=by_channel_tile(tilt))
        load_s(1)
        load_q(1)
        load_q(2)

        table_probe = keep.tile([P, 2], F32, name="table_probe")
        nc.vector.memset(table_probe[:, 0:1], 1.0)
        nc.scalar.activation(out=table_probe[:, 1:2], in_=table_probe[:, 0:1], func=ACT.Abs_reciprocal_sqrt)

        piece_a = keep.tile([P, 4, 16, 8, 2], BF16, name="piece_a")
        piece_b = keep.tile([P, 4, 16, 8, 2], BF16, name="piece_b")
        words_a = piece_a[:].bitcast(F32).rearrange("p c l s o -> p c l (s o)")
        words_b = piece_b[:].bitcast(F32).rearrange("p c l s o -> p c l (s o)")
        upper, lower, both_runs = slice(0, 4), slice(4, 8), slice(0, 8)

        nc.vector.memset(us_raw[:].bitcast(I32), 0)
        for table in (piece_b, piece_a):
            nc.vector.memset(table[:].rearrange("p c l s e -> p (c l s e)").bitcast(I32), 0)
        for table, levels, slot, value in (
            (piece_b, both_runs, 0, 1.0),
            (piece_b, upper, 3, 2.0),
            (piece_b, lower, 3, 1.0),
            (piece_b, lower, 5, 1.0),
            (piece_a, upper, 4, 1.0),
            (piece_a, upper, 7, 2.0),
            (piece_a, lower, 7, 1.0),
        ):
            nc.vector.memset(table[:, :, levels, slot, :], value)

        nc.sync.dma_start(out=uw_raw[:].bitcast(I32), in_=u_words.rearrange("g p n -> p g n").bitcast(I32))
        for quad in range(4):
            nc.sync.dma_start(
                out=us_raw[32 * quad : 32 * quad + 4].bitcast(I32),
                in_=u_scales[:, 4 * quad : 4 * quad + 4, :].rearrange("g r n -> r g n").bitcast(I32),
            )
        load_s(2)
        load_q(3)
        load_s(3)

        lam_pairs = lam_c[:].rearrange("p (c e) -> p c e", e=2)
        for table, levels, slot in ((piece_b, both_runs, 1), (piece_b, lower, 4), (piece_a, upper, 5)):
            nc.scalar.activation(
                out=table[:, :, levels, slot, :],
                in_=lam_pairs.unsqueeze(2).to_broadcast([P, 4, levels.stop - levels.start, 2]),
                func=ACT.Copy,
                scale=-4.0,
            )

        scale_row = keep.tile([P, N], F32, name="scale_row")
        for g in range(2):
            spread = take_bank(("scale", g), [P, 4, P])
            for t in range(4):
                nc.tensor.transpose(spread[:, t, :], scale_c[:, 4 * g + t : 4 * g + t + 1].to_broadcast([P, P]), ident[:])

        base = keep.tile([P, 3, TILES], F32, name="base")
        halves = keep.tile([P, 2, 2, TILES], BF16, name="halves")
        whole = keep.tile([P, 10, TILES], F32, name="whole")
        remainder = keep.tile([P, 10, TILES], F32, name="remainder")
        pieces = keep.tile([P, 3, 10, TILES], BF16, name="pieces")
        lam32 = keep.tile([P, TILES], F32, name="lam32")
        lam_part = keep.tile([P, 1], F32, name="lam_part")
        inv_lam = keep.tile([P, TILES], F32, name="inv_lam")
        arg_scale = keep.tile([P, TILES], F32, name="arg_scale")
        arg_bias = keep.tile([P, TILES], F32, name="arg_bias")
        h_lam = keep.tile([P, TILES], F32, name="h_lam")

        nc.vector.tensor_tensor(out=base[:, 1, :], in0=lam_c[:], in1=lam_c[:], op=ALU.mult)
        nc.vector.scalar_tensor_tensor(out=base[:, 0, :], in0=lam_c[:], scalar=2.0 * H * H, in1=lam_c[:], op0=ALU.mult, op1=ALU.mult)
        nc.vector.tensor_scalar(out=base[:, 2, :], in0=lam_c[:], scalar1=0.5, scalar2=None, op0=ALU.mult)
        nc.vector.tensor_scalar(out=lam32[:], in0=lam_c[:], scalar1=1.0, scalar2=None, op0=ALU.mult, op1=ALU.add, accum_out=lam_part[:])
        nc.vector.tensor_copy(out=halves[:, 0], in_=base[:, 0:2, :])
        nc.vector.tensor_tensor(out=whole[:, 1, :], in0=base[:, 1, :], in1=lam_c[:], op=ALU.mult)
        nc.vector.tensor_scalar(out=whole[:, 2, :], in0=base[:, 1, :], scalar1=6.0, scalar2=None, op0=ALU.mult)
        nc.vector.tensor_tensor(out=halves[:, 1], in0=base[:, 0:2, :], in1=halves[:, 0], op=ALU.subtract)
        nc.vector.reciprocal(out=inv_lam[:], in_=lam32[:])
        nc.vector.tensor_scalar(out=arg_bias[:], in0=base[:, 1, :], scalar1=(H * H * N / CONC) ** 2, scalar2=None, op0=ALU.mult)
        nc.vector.tensor_tensor(out=whole[:, 0:7:6, :], in0=halves[:, 0:1, 1, :].to_broadcast([P, 2, TILES]), in1=halves[:, :, 1, :], op=ALU.mult)
        nc.vector.tensor_tensor(out=whole[:, 9, :], in0=halves[:, 1, 1, :], in1=halves[:, 1, 1, :], op=ALU.mult)
        nc.vector.tensor_tensor(
            out=whole[:, 3:9, :].rearrange("p (i j) c -> p i j c", j=2)[:, 0:3:2],
            in0=halves[:, :, 0:1, :].to_broadcast([P, 2, 2, TILES]),
            in1=base[:, 1:3, :].unsqueeze(1).to_broadcast([P, 2, 2, TILES]),
            op=ALU.mult,
        )
        nc.vector.tensor_tensor(out=whole[:, 5, :], in0=halves[:, 0, 0, :], in1=halves[:, 1, 0, :], op=ALU.add)
        nc.vector.tensor_copy(
            out=words_b[:, :, both_runs, 2:7:4],
            in_=halves[:, :, 1, :].bitcast(F32).rearrange("p s c -> p c s").unsqueeze(2).to_broadcast([P, 4, 8, 2]),
        )
        nc.vector.tensor_copy(out=pieces[:, 0], in_=whole[:])
        nc.vector.scalar_tensor_tensor(out=arg_scale[:], in0=inv_lam[:], scalar=(N / CONC) ** 2, in1=inv_lam[:], op0=ALU.mult, op1=ALU.mult)
        nc.vector.tensor_scalar(out=h_lam[:], in0=lam_c[:], scalar1=H, scalar2=None, op0=ALU.mult)
        nc.vector.tensor_tensor(out=pieces[:, 1], in0=whole[:], in1=pieces[:, 0], op=ALU.subtract)
        nc.vector.tensor_tensor(out=remainder[:], in0=whole[:], in1=pieces[:, 0], op=ALU.subtract)
        nc.vector.tensor_tensor(out=pieces[:, 2], in0=remainder[:], in1=pieces[:, 1], op=ALU.subtract)

        for g in range(2):
            nc.scalar.copy(
                out=scale_row[:, PASS * g : PASS * (g + 1)].rearrange("p (n t) -> p n t", t=4),
                in_=in_psum[("scale", g)][0][:].rearrange("p t n -> p n t"),
            )
            give_bank(("scale", g))

        piece_words = pieces[:].bitcast(F32).rearrange("p l q c -> p c l q")
        nc.vector.tensor_copy(out=words_b[:, :, 0:3, 4:6], in_=piece_words[:, :, :, 0:2])
        nc.vector.tensor_copy(
            out=words_b[:, :, both_runs, 7].rearrange("p c (k l) -> p c k l", k=2)[:, :, :, 1:4],
            in_=piece_words[:, :, :, 6:10:3].rearrange("p c l k -> p c k l"),
        )
        nc.scalar.copy(
            out=words_a[:, :, both_runs, 0:3].rearrange("p c (k l) s -> p c k l s", k=2)[:, :, :, 0:3, :],
            in_=piece_words[:, :, :, 0:6].rearrange("p c l (k s) -> p c k l s", k=2),
        )
        nc.scalar.copy(out=words_a[:, :, 5:8, 3:6], in_=piece_words[:, :, :, 7:10])
        nc.scalar.copy(
            out=words_a[:, :, both_runs, 6].rearrange("p c (k l) -> p c k l", k=2)[:, :, :, 1:4],
            in_=piece_words[:, :, :, 2:6:3].rearrange("p c l k -> p c k l"),
        )
        nc.scalar.copy(out=words_a[:, :, 1:4, 3], in_=piece_words[:, :, :, 6])

        s_wide = [keep.tile([P, N], BF16, name="s_wide%d" % r) for r in range(TILES)]
        grouped, codes, scales = {}, {}, {}
        for kind in ("q", "s"):
            grouped[kind] = [keep.tile([P, 2, PAIR, 2], F32, name="%s_grouped%d" % (kind, d), tag="%s_grouped%d" % (kind, d), align_bytes=64) for d in range(4)]
            codes[kind] = [keep.tile([P, 2, PASS], U32, name="%s_codes%d" % (kind, half), align_bytes=64) for half in range(2)]
            scales[kind] = [keep.tile([P, 2, PASS], U8, name="%s_scales%d" % (kind, half), align_bytes=64) for half in range(2)]

        def widen(r, lo=0, hi=N):
            nc.vector.tensor_tensor(out=s_wide[r][:, lo:hi], in0=s_raw[r // 2][:, r % 2, lo:hi].bitcast(FP8), in1=scale_row[:, lo:hi], op=ALU.mult)

        def turn_words(dst, rows, g, u):
            nc.tensor.transpose(dst, rows.bitcast(F32)[:, 256 * g + u : 256 * (g + 1) : 2], ident[:])

        def turn(kind, r):
            rows = q_raw[r // 2][:, r % 2, :] if kind == "q" else s_wide[r][:]
            turned = take_bank((kind, r), [P, 2, 2, P])
            for g in range(2):
                for u in range(2):
                    turn_words(turned[:, g, u, :], rows, g, u)

        def group(kind, r, on_vector=False):
            copy_on(on_vector)(
                out=grouped[kind][r // 2][:, :, P * (r % 2) : P * (r % 2 + 1), :],
                in_=in_psum[(kind, r)][0][:].rearrange("p g u r -> p g r u"),
            )
            give_bank((kind, r))

        def quantise(kind, d, g):
            cols = slice(PAIR * (d % 2), PAIR * (d % 2 + 1))
            nc.vector.quantize_mx(
                out=codes[kind][d // 2][:, g, cols].bitcast(FP8X4),
                scales=scales[kind][d // 2][:, g, cols],
                in_=grouped[kind][d][:, g].rearrange("p r u -> p (r u)").bitcast(BF16),
            )

        turn("q", 0)
        group("q", 0)
        for r in range(3):
            widen(r)

        rows_a = keep.tile([P, 4, P], F32, name="rows_a")
        rows_b = keep.tile([P, 4, P], F32, name="rows_b")
        for words, rows, lo, hi in ((words_b, rows_b, 0, 2), (words_a, rows_a, 0, 1), (words_b, rows_b, 2, 4), (words_a, rows_a, 1, 4)):
            turned_table = take_bank("table", [P, hi - lo, P])
            for cp in range(lo, hi):
                nc.tensor.transpose(turned_table[:, cp - lo, :], words[:, cp].rearrange("p l s -> p (l s)"), ident[:])
            nc.scalar.copy(out=rows[:, lo:hi], in_=turned_table[:])
            give_bank("table")
        pair_moving = rows_b[:].rearrange("p c n -> p (c n)").bitcast(BF16)
        pair_stationary = rows_a[:].bitcast(BF16)

        lam_spread = take_bank("lam", [P, 4, P])
        for cp in range(4):
            nc.tensor.transpose(lam_spread[:, cp, :], lam_c[:].bitcast(F32)[:, cp : cp + 1].to_broadcast([P, P]), ident[:])
        lam_row = lam_spread[:].rearrange("p c n -> p (c n)").bitcast(BF16)

        def sum_over_partitions(key, column):
            total = take_bank(key, [P, 1])
            nc.tensor.matmul(total[:], lhsT=ones[:], rhs=column, start=True, stop=True)
            return total

        inv_lam_sum = keep.tile([P, 1], F32, name="inv_lam_sum")
        weight = keep.tile([P, TILES], F32, name="weight")
        nc.vector.reciprocal(out=inv_lam_sum[:], in_=sum_over_partitions("lam_sum", lam_part[:])[:])
        give_bank("lam_sum")
        widen(3)
        nc.vector.scalar_tensor_tensor(out=weight[:], in0=tilt_c[:], scalar=inv_lam_sum[:], in1=inv_lam[:], op0=ALU.mult, op1=ALU.mult)

        u_codes, u_planes = {}, {}

        def order_u_words(gx, slot):
            u_codes[gx] = keep.tile([P, 2, N], U8, name="u_codes%d" % gx, tag=slot, align_bytes=64)
            nc.gpsimd.tensor_copy(
                out=u_codes[gx][:].rearrange("p g (t m b) -> p g t m b", t=4, b=2),
                in_=uw_raw[:, :, N * gx : N * (gx + 1)].rearrange("p g (m t b) -> p g t m b", t=4, b=2),
            )

        def order_u_scales(gx, slot):
            u_planes[gx] = keep.tile([P, 2, PASS], U8, name="u_planes%d" % gx, tag=slot, align_bytes=64)
            nc.gpsimd.tensor_copy(
                out=u_planes[gx][:].rearrange("p g (t m) -> p g t m", t=4),
                in_=us_raw[:, :, PASS * gx : PASS * (gx + 1)].rearrange("p g (m t) -> p g t m", t=4),
            )

        order_u_words(0, "tilt_then_u")
        order_u_scales(0, "u_planes0")
        order_u_words(1, "u_codes1")

        row_sums = keep.tile([P, TILES, 2], F32, name="row_sums")
        skew_sums = keep.tile([P, TILES], F32, name="skew_sums")
        inv_den = {}

        def invert_pairs(c):
            inv_den[c] = ring.tile([P, N], F32, name="inv_den", bufs=4)
            for part in range(2):
                cols = slice(PASS * part, PASS * (part + 1))
                square = take_bank("pairs", [P, PASS])
                nc.tensor.matmul(square[:], lhsT=pair_stationary[:, c // 2, c % 2 :: 2], rhs=pair_moving[:, cols], start=True, stop=True)
                nc.scalar.activation(
                    out=inv_den[c][:, cols],
                    in_=square[:],
                    func=ACT.Abs_reciprocal_sqrt,
                    scale=arg_scale[:, c : c + 1],
                    bias=arg_bias[:, c : c + 1],
                    accum_out=row_sums[:, c, part : part + 1],
                )
                give_bank("pairs")

        def skew(c):
            nc.vector.scalar_tensor_tensor(
                out=inv_den[c][:],
                in0=lam_row,
                scalar=lam32[:, c : c + 1],
                in1=inv_den[c][:],
                op0=ALU.subtract,
                op1=ALU.mult,
                accum_out=skew_sums[:, c : c + 1],
            )

        for c in range(TILES):
            invert_pairs(c)
            if 2 <= c < 6:
                group("s", c - 2, on_vector=(c == 2))
            turn(*(("s", c) if c < 4 else ("q", c - 3)))
            if c >= 1:
                skew(c - 1)
            if c == TILES - 2:
                for g in range(2):
                    for d in range(2):
                        quantise("s", d, g)
                order_u_scales(1, "s_grouped1")
        skew(TILES - 1)

        factor = keep.tile([P, TILES], F32, name="factor")
        x_planes = [[keep.tile([P, 4, PASS], BF16, name="x_planes%d%d" % (half, gx)) for gx in range(2)] for half in range(2)]
        x_codes = [keep.tile([P, 2, PAIR], U32, name="x_codes%d" % d, align_bytes=64) for d in range(4)]
        x_scales = [keep.tile([P, 2, PAIR], U8, name="x_scales%d" % d, align_bytes=64) for d in range(4)]
        x_grouped, result = {}, {}
        out_rows = out.rearrange("(d p a) t -> d a p t", p=P, a=2)

        def first(half, c, passes=(0, 1)):
            if 0 in passes:
                take_bank(("y", half, c), [P, PASS])
            for g in passes:
                nc.tensor.matmul_mx(
                    in_psum[("y", half, c)][0][:],
                    lhsT=u_codes[c // 4][:, g, 2 * P * (c % 4) : 2 * P * (c % 4 + 1)].bitcast(FP4X4),
                    lhsT_scale=u_planes[c // 4][:, g, P * (c % 4) : P * (c % 4 + 1)],
                    rhs=codes["s"][half][:, g, :].bitcast(FP8X4),
                    rhs_scale=scales["s"][half][:, g, :],
                    start=(g == 0),
                    stop=(g == 1),
                )

        def shrink(half, c, on_vector=False):
            plane, y, column = x_planes[half][c // 4][:, c % 4, :], in_psum[("y", half, c)][0][:], factor[:, c : c + 1]
            if on_vector:
                nc.vector.tensor_scalar(out=plane, in0=y, scalar1=column, scalar2=None, op0=ALU.mult)
            else:
                nc.scalar.activation(out=plane, in_=y, func=ACT.Copy, scale=column)
            give_bank(("y", half, c))

        def weave(d, gx):
            x_grouped[(d, gx)] = ring.tile([P, PAIR, 4], BF16, name="x_grouped", align_bytes=64)
            planes = x_planes[d // 2][gx][:, :, PAIR * (d % 2) : PAIR * (d % 2 + 1)]
            nc.vector.tensor_copy(out=x_grouped[(d, gx)][:], in_=planes.rearrange("p t n -> p n t"))

        def quantise_x(d, gx):
            nc.vector.quantize_mx(
                out=x_codes[d][:, gx, :].bitcast(FP8X4),
                scales=x_scales[d][:, gx, :],
                in_=x_grouped[(d, gx)][:].rearrange("p n t -> p (n t)"),
            )

        def second(r, lo, width):
            tokens = slice(P * (r % 2), P * (r % 2 + 1))
            cols = slice(lo % PASS, lo % PASS + width)
            acc = take_bank(("out", r, lo), [P, width])
            for gx in range(2):
                nc.tensor.matmul_mx(
                    acc[:],
                    lhsT=x_codes[r // 2][:, gx, tokens].bitcast(FP8X4),
                    lhsT_scale=x_scales[r // 2][:, gx, tokens],
                    rhs=codes["q"][lo // PASS][:, gx, cols].bitcast(FP8X4),
                    rhs_scale=scales["q"][lo // PASS][:, gx, cols],
                    start=(gx == 0),
                    stop=(gx == 1),
                )

        def empty(r, lo, width, on_vector=False):
            if lo == 0:
                result[r] = ring.tile([P, N], F32, name="result", bufs=6)
            copy_on(on_vector)(out=result[r][:, lo : lo + width], in_=in_psum[("out", r, lo)][0][:])
            give_bank(("out", r, lo))

        def store(r, lo, width):
            nc.sync.dma_start(out=out_rows[r // 2, r % 2, :, lo : lo + width], in_=result[r][:, lo : lo + width])

        for g in range(2):
            for c in range(3):
                first(0, c, (g,))
        group("q", 1)
        group("q", 2)
        turn("q", 5)
        turn("q", 6)
        group("q", 3)
        group("q", 4)
        first(0, 3)
        turn("q", 7)
        group("q", 5)
        first(0, 4)
        group("q", 6)
        give_bank("lam")
        group("q", 7)

        row_sum = keep.tile([P, TILES], F32, name="row_sum")
        legs = keep.tile([P, 2, TILES], F32, name="legs")
        squares = keep.tile([P, 2, TILES], F32, name="squares")
        g_vals = keep.tile([P, TILES], F32, name="g_vals")
        inv_g = keep.tile([P, TILES], F32, name="inv_g")
        r_vals = keep.tile([P, TILES], F32, name="r_vals")
        r_part = keep.tile([P, 1], F32, name="r_part")
        unscaled = keep.tile([P, TILES], F32, name="unscaled")
        quarter = N // 4
        nc.vector.tensor_tensor(out=row_sum[:], in0=row_sums[:, :, 0], in1=row_sums[:, :, 1], op=ALU.add)
        nc.vector.tensor_scalar(out=legs[:, 0, :], in0=skew_sums[:], scalar1=CONC - 1.0, scalar2=None, op0=ALU.add)
        widen(4, 0, quarter)
        nc.vector.tensor_tensor(out=legs[:, 1, :], in0=row_sum[:], in1=h_lam[:], op=ALU.mult)
        widen(4, quarter, 2 * quarter)
        nc.vector.tensor_tensor(out=squares[:], in0=legs[:], in1=legs[:], op=ALU.mult)
        widen(4, 2 * quarter, 3 * quarter)
        nc.vector.tensor_tensor(out=g_vals[:], in0=squares[:, 0, :], in1=squares[:, 1, :], op=ALU.add)
        widen(4, 3 * quarter, N)
        nc.vector.reciprocal(out=inv_g[:], in_=g_vals[:])
        widen(5, 0, quarter)
        nc.vector.scalar_tensor_tensor(out=r_vals[:], in0=inv_g[:], scalar=1.0, in1=lam32[:], op0=ALU.mult, op1=ALU.mult, accum_out=r_part[:])
        nc.vector.tensor_tensor(out=unscaled[:], in0=g_vals[:], in1=weight[:], op=ALU.mult)
        r_total = sum_over_partitions("r_sum", r_part[:])
        widen(5, quarter, N)
        nc.vector.tensor_scalar(out=factor[:], in0=unscaled[:], scalar1=r_total[:], scalar2=None, op0=ALU.mult)
        give_bank("r_sum")
        widen(6)
        widen(7)

        first(0, 5)
        turn("s", 4)
        turn("s", 5)
        shrink(0, 0)
        shrink(0, 1)
        first(0, 6)
        group("s", 4)
        group("s", 5)
        last_pair = [take_bank(("pass", g), [P, 2, 2, P]) for g in range(2)]
        for a in range(2):
            for g in range(2):
                for u in range(2):
                    turn_words(last_pair[g][:, u, a, :], s_wide[6 + a][:], g, u)
        shrink(0, 2)
        first(0, 7)
        for kind, d in (("q", 0), ("s", 2)):
            for g in range(2):
                quantise(kind, d, g)
        for g in range(2):
            copy_on(g == 1)(out=grouped["s"][3][:, g], in_=last_pair[g][:].rearrange("p u a r -> p (a r) u"))
            give_bank(("pass", g))
        for g in range(2):
            quantise("s", 3, g)
        for c in (3, 4, 5, 7):
            shrink(0, c)
        quantise("q", 1, 0)
        quantise("q", 1, 1)
        weave(0, 0)
        quantise("q", 2, 0)
        quantise("q", 2, 1)
        shrink(0, 6, on_vector=True)
        weave(0, 1)
        for g in range(2):
            quantise_x(0, g)
            quantise("q", 3, g)
        for step in (weave, quantise_x):
            for gx in range(2):
                step(1, gx)

        for g in range(2):
            for c in range(2):
                first(1, c, (g,))
        for c in range(2, TILES):
            first(1, c)
        for c in range(TILES - 1):
            shrink(1, c)
        weave(2, 0)
        second(0, 0, PASS)
        empty(0, 0, PASS)
        store(0, 0, PASS)
        shrink(1, TILES - 1, on_vector=True)
        weave(2, 1)
        for step, d in ((quantise_x, 2), (weave, 3), (quantise_x, 3)):
            for gx in range(2):
                step(d, gx)
        second(0, PASS, PASS)
        empty(0, PASS, PASS)
        store(0, PASS, PASS)
        for r in range(1, TILES - 1):
            for lo in (0, PASS):
                second(r, lo, PASS)
                empty(r, lo, PASS, on_vector=(r >= 4 and lo == PASS))
            store(r, 0, N)
        last = TILES - 1
        second(last, 0, PASS)
        second(last, PASS, PASS // 2)
        second(last, PASS + PASS // 2, PASS // 2)
        empty(last, 0, PASS)
        store(last, 0, PASS)
        empty(last, PASS, PASS // 2, on_vector=True)
        empty(last, PASS + PASS // 2, PASS // 2)
        store(last, PASS, PASS)
